import numpy as np
import ml_dtypes


def mxq(x, axis, fmt="e4m3"):
    dtype, down = {"e4m3": (ml_dtypes.float8_e4m3fn, 7), "e5m2": (ml_dtypes.float8_e5m2, 14)}[fmt]
    v = np.moveaxis(np.asarray(x, np.float32).astype(ml_dtypes.bfloat16).astype(np.float64), axis, -1)
    blocks = v.reshape(v.shape[:-1] + (-1, 32))
    amax = np.abs(blocks).max(-1, keepdims=True)
    byte = np.maximum(np.where(amax > 0, np.frexp(amax)[1] - 1 + 127, 0) - down, 1)
    scale = np.exp2(byte - 127.0)
    codes = (blocks / scale).astype(np.float32).astype(dtype).astype(np.float64)
    return np.moveaxis((codes * scale).reshape(v.shape), -1, axis)


WIDE = False


def mx_kscale(k):
    if not WIDE:
        return np.ones(k)
    levels = np.array([10, -10, 5, -5, 0])
    if k % 512:
        return np.exp2(np.random.permutation(np.resize(levels, k // 32))).repeat(32)
    a = np.empty((k // 512, 16))
    for p in range(k // 512):
        a[p, :8] = np.random.permutation(np.resize(levels, 8))
        for g in range(8):
            far = levels[np.abs(levels - a[p, g]) >= 10]
            a[p, g + 8] = far[np.random.randint(len(far))]
    return np.exp2(a.ravel()).repeat(32)


def f64(x):
    return np.asarray(x).astype(np.float64)


def striped(idx):
    return np.tile(idx.reshape(-1, 16).T, (8, 1)).astype(np.uint16)


def unstriped(offs):
    return offs[:16].T.reshape(-1).astype(np.int64)


def pack_weight(w):
    k, n = w.shape
    w = f64(np.asarray(w, np.float32).astype(ml_dtypes.bfloat16)).reshape(k // 32, 32, n)
    amax = np.abs(w).max(1)
    byte = np.clip(np.where(amax > 0, np.frexp(amax)[1] - 1 + 127 - 7, 1), 1, 254)
    scaled = (w * np.exp2(127.0 - byte)[:, None, :]).reshape(k, n).astype(np.float32)
    words = np.ascontiguousarray(scaled.reshape(k // 512, 128, 4, n).transpose(0, 1, 3, 2)).astype(ml_dtypes.float8_e4m3fn).view(np.uint8)
    return words, np.ascontiguousarray(byte.astype(np.uint8).reshape(k // 512, 16, n))


def unpack_weight(words, scales):
    g, p, n, _ = words.shape
    vals = np.ascontiguousarray(words).view(ml_dtypes.float8_e4m3fn).astype(np.float64) * np.repeat(np.exp2(scales.astype(np.float64) - 127.0), 8, axis=1)[..., None]
    return vals.transpose(0, 1, 3, 2).reshape(g * 512, n)

def planes(y):
    n, m = y.shape
    v = y.astype(np.float32).astype(ml_dtypes.bfloat16).astype(np.float64).reshape(n // 32, 32, m)
    top = np.abs(v).max(1)
    byte = np.clip(np.where(top > 0, np.frexp(top)[1] - 1 + 127 - 7, 1), 1, 254)
    codes = (v * np.exp2(127.0 - byte)[:, None, :]).reshape(n, m).astype(np.float32).astype(ml_dtypes.float8_e4m3fn).view(np.uint8)
    words = codes.reshape(n // 512, 128, 4, m).transpose(0, 1, 3, 2)
    return np.ascontiguousarray(words), np.ascontiguousarray(byte.astype(np.uint8).reshape(n // 512, 16, m))


K, T, N, U = 512, 512, 512, 1024
P = 2 ** 7


def setup_inputs():
    n = np.random.standard_normal
    s = mx_kscale(K)[:, None]
    packed_xT = pack_weight(n((K, T)) * s)
    return {
        "x_words": packed_xT[0],
        "x_scales": packed_xT[1],
        "mem": n((N, U)).astype(np.float32),
        "w1": (n((K, N)) / np.sqrt(K) / s).astype(np.float32),
        "old": np.tile(np.random.uniform(0.5, 0.95, T), (P, 1)).astype(np.float32),
        "new": np.tile(np.random.uniform(0.05, 0.5, T), (P, 1)).astype(np.float32),
        "slot": striped(np.random.permutation(U)[:T]),
    }


def reference(x_words, x_scales, mem, w1, old, new, slot):
    xq = unpack_weight(x_words, x_scales)
    y = np.tanh(mxq(f64(w1), 0, "e4m3").T @ xq)
    out = f64(mem).copy()
    out[:, unstriped(slot)] = f64(mem)[:, unstriped(slot)] * f64(old)[:1] + y * f64(new)[:1]
    return (out,) + planes(out)

@@ -1,0 +1,167 @@
+from contextlib import ExitStack
+
+import concourse.mybir as mybir
+from concourse.masks import make_identity
+
+K, T, N, U = 512, 512, 512, 1024
+P = 128
+PACK = 4
+QUAD = 32
+QUARTER = U // 4
+
+F32 = mybir.dt.float32
+BF16 = mybir.dt.bfloat16
+I32 = mybir.dt.int32
+U32 = mybir.dt.uint32
+U16 = mybir.dt.uint16
+U8 = mybir.dt.uint8
+FP8X4 = mybir.dt.float8_e4m3fn_x4
+MULT = mybir.AluOpType.mult
+ADD = mybir.AluOpType.add
+TANH = mybir.ActivationFunctionType.Tanh
+
+FLOPS = 2 * K * N * T
+BYTES = K * T + K * T // 32 + 4 * N * U + 4 * K * N + 2 * 4 * T + 2 * P * T // 16 + 4 * N * U + N * U + N * U // 32
+
+
+def tile_picked_wema_tanh_lo_kernel(
+    tc, x_words, x_scales, mem, w1, old, new, slot, out_0, out_1, out_2
+):
+    nc = tc.nc
+    mem_rows = mem.rearrange("(p t) u -> p t u", t=PACK)
+    out_rows = out_0.rearrange("(p t) u -> p t u", t=PACK)
+
+    with ExitStack() as ctx:
+        keep = ctx.enter_context(tc.tile_pool(name="keep", bufs=1))
+        psum = ctx.enter_context(tc.psum_pool(name="psum", bufs=1))
+
+        offsets = keep.tile([P, T // 16], U16, name="offsets")
+        window = [keep.tile([P, U], F32, name=f"window{t}") for t in range(PACK)]
+        w_raw = keep.tile([P, PACK, N], F32, name="w_raw")
+        x_codes = keep.tile([P, T], U32, name="x_codes", align_bytes=64)
+        x_plane = keep.tile([P, T], U8, name="x_plane", align_bytes=64)
+        old_cols = keep.tile([P, PACK], F32, name="old_cols")
+        new_cols = keep.tile([P, PACK], F32, name="new_cols")
+        identity = keep.tile([P, P], F32, name="identity")
+        warm_in = keep.tile([P, 1], F32, name="warm_in")
+        warm_out = keep.tile([P, 1], F32, name="warm_out")
+
+        nc.vector.memset(x_plane[:].bitcast(I32), 0)
+        nc.sync.dma_start(old_cols[:], old[0, :].rearrange("(p i) -> p i", i=PACK))
+        nc.scalar.dma_start(new_cols[:], new[0, :].rearrange("(p i) -> p i", i=PACK))
+        nc.sync.dma_start(window[0][:], mem_rows[:, 0, :])
+        nc.sync.dma_start(offsets[:], slot)
+        nc.sync.dma_start(window[1][:], mem_rows[:, 1, :])
+        nc.sync.dma_start(w_raw[:], w1.rearrange("(p j) n -> p j n", j=PACK))
+        nc.sync.dma_start(x_codes[:].bitcast(I32), x_words[0].rearrange("p n j -> p (n j)").bitcast(I32))
+        for q in range(P // QUAD):
+            nc.sync.dma_start(
+                x_plane[QUAD * q : QUAD * q + 4, :].bitcast(I32), x_scales[0, 4 * q : 4 * q + 4, :].bitcast(I32)
+            )
+        for t in range(2, PACK):
+            nc.sync.dma_start(window[t][:], mem_rows[:, t, :])
+
+        nc.vector.memset(warm_in[:], 0.0)
+        nc.scalar.activation(warm_out[:], warm_in[:], TANH)
+
+        make_identity(nc, identity[:])
+
+        def spread(cols, label):
+            bank = psum.tile([P, PACK, P], F32, name=f"{label}_bank")
+            for i in range(PACK):
+                nc.tensor.transpose(bank[:, i, :], cols[:, i : i + 1].to_broadcast([P, P]), identity[:])
+            return bank
+
+        def rows_of(bank, label, tag, copy):
+            rows = keep.tile([P, T], F32, name=label, tag=tag, align_bytes=64)
+            copy(rows[:].rearrange("p (n i) -> p n i", i=PACK), bank[:].rearrange("p i n -> p n i"))
+            return rows
+
+        old_bank = spread(old_cols, "old")
+        new_bank = spread(new_cols, "new")
+        old_first = rows_of(old_bank, "old_first", "rest", nc.vector.tensor_copy)
+        old_early = rows_of(old_bank, "old_early", "head", nc.scalar.copy)
+        old_late = rows_of(old_bank, "old_late", "blend", nc.scalar.copy)
+        new_rows = rows_of(new_bank, "new_rows", "new_rows", nc.scalar.copy)
+
+        kept = {}
+
+        def look_up(t, old_rows, tag):
+            kept[t] = keep.tile([P, T], F32, name=f"kept{t}", tag=tag, align_bytes=64)
+            nc.vector.tensor_tensor(kept[t][:], window[t][:].indirect(offsets[:]), old_rows[:], MULT)
+
+        look_up(0, old_first, "kept0")
+        look_up(1, old_early, "kept1")
+
+        w_dealt = w_raw[:].rearrange("p j (m t) -> p m j t", t=PACK)
+        w_first = keep.tile([P, P * PACK], BF16, name="w_first", tag="head", align_bytes=64)
+        w_rest = keep.tile([P, (PACK - 1) * P * PACK], BF16, name="w_rest", tag="rest", align_bytes=64)
+        w_codes = [keep.tile([P, P], U32, name="w_codes0", align_bytes=64), keep.tile([P, 3 * P], U32, name="w_codes1", align_bytes=64)]
+        w_plane = [keep.tile([P, P], U8, name="w_plane0", align_bytes=64), keep.tile([P, 3 * P], U8, name="w_plane1", align_bytes=64)]
+        nc.vector.tensor_copy(w_first[:].rearrange("p (m j) -> p m j", j=PACK), w_dealt[:, :, :, 0])
+        nc.scalar.copy(w_rest[:].rearrange("p (t m j) -> p m j t", t=PACK - 1, j=PACK), w_dealt[:, :, :, 1:PACK])
+        nc.vector.quantize_mx(w_codes[0][:].bitcast(FP8X4), w_plane[0][:], w_first[:])
+
+        y = [keep.tile([P, T], F32, name=f"y{t}") for t in range(PACK)]
+
+        def project(t):
+            part, cols = (0, slice(0, P)) if t == 0 else (1, slice((t - 1) * P, t * P))
+            acc = psum.tile([P, T], F32, name=f"acc{t}")
+            nc.tensor.matmul_mx(
+                out=acc[:],
+                lhsT=w_codes[part][:, cols].bitcast(FP8X4),
+                lhsT_scale=w_plane[part][:, cols],
+                rhs=x_codes[:].bitcast(FP8X4),
+                rhs_scale=x_plane[:],
+                start=True,
+                stop=True,
+            )
+            nc.scalar.activation(y[t][:], acc[:], TANH)
+
+        project(0)
+        look_up(2, old_late, "head")
+        nc.vector.quantize_mx(w_codes[1][:, 0:P].bitcast(FP8X4), w_plane[1][:, 0:P], w_rest[:, 0 : P * PACK])
+        nc.vector.quantize_mx(w_codes[1][:, P : 3 * P].bitcast(FP8X4), w_plane[1][:, P : 3 * P], w_rest[:, P * PACK : 3 * P * PACK])
+        for t in range(1, PACK):
+            project(t)
+        look_up(3, old_late, "kept3")
+
+        grouped = [keep.tile([P, QUARTER, PACK], BF16, name=f"grouped{c}", align_bytes=64) for c in range(4)]
+        codes = keep.tile([P, U], U32, name="codes", align_bytes=64)
+        plane = keep.tile([P, U], U8, name="plane", align_bytes=64)
+
+        def cols_of(c):
+            return slice(c * QUARTER, (c + 1) * QUARTER)
+
+        for t in range(PACK):
+            engine = nc.vector if t == 0 else nc.gpsimd
+            fresh = keep.tile([P, T], F32, name="fresh", tag="blend", align_bytes=64)
+            moved = keep.tile([P, T], F32, name=f"moved{t}")
+            engine.tensor_tensor(fresh[:], y[t][:], new_rows[:], MULT)
+            engine.tensor_tensor(moved[:], kept[t][:], fresh[:], ADD)
+            nc.vector.tensor_copy(window[t][:].indirect(offsets[:]), moved[:])
+            nc.sync.dma_start(out_rows[:, t, :], window[t][:])
+            if t < PACK - 1:
+                for c in range(4):
+                    nc.scalar.copy(grouped[c][:, :, t], window[t][:, cols_of(c)])
+                    if t == PACK - 2 and c < 2:
+                        last = (c + 1) * QUARTER - 1
+                        nc.scalar.copy(
+                            grouped[c][:, QUARTER - 1, t : t + 2], window[t][:, last : last + 1].to_broadcast([P, 2])
+                        )
+
+        t = PACK - 1
+        for c in range(4):
+            if c < 2:
+                nc.vector.tensor_copy(grouped[c][:, :, t], window[t][:, cols_of(c)])
+            else:
+                nc.scalar.copy(grouped[c][:, :, t], window[t][:, cols_of(c)])
+        words = out_1[0].rearrange("p u j -> p (u j)").bitcast(I32)
+        for c in range(4):
+            nc.vector.quantize_mx(
+                codes[:, cols_of(c)].bitcast(FP8X4), plane[:, cols_of(c)], grouped[c][:].rearrange("p u j -> p (u j)")
+            )
+            nc.sync.dma_start(words[:, cols_of(c)], codes[:, cols_of(c)].bitcast(I32))
+        for q in range(P // QUAD):
+            queue = nc.scalar if q % 2 == 0 else nc.sync
+            queue.dma_start(out_2[0, 4 * q : 4 * q + 4, :].bitcast(I32), plane[QUAD * q : QUAD * q + 4, :].bitcast(I32))

@@ -7,7 +7,6 @@ K, T, N, U = 512, 512, 512, 1024
 P = 128
 PACK = 4
 QUAD = 32
-QUARTER = U // 4
 
 F32 = mybir.dt.float32
 BF16 = mybir.dt.bfloat16
@@ -81,8 +80,9 @@ def tile_picked_wema_tanh_lo_kernel(
         new_bank = spread(new_cols, "new")
         old_first = rows_of(old_bank, "old_first", "rest", nc.vector.tensor_copy)
         old_early = rows_of(old_bank, "old_early", "head", nc.scalar.copy)
-        old_late = rows_of(old_bank, "old_late", "blend", nc.scalar.copy)
+        old_late = rows_of(old_bank, "old_late", "late", nc.scalar.copy)
         new_rows = rows_of(new_bank, "new_rows", "new_rows", nc.scalar.copy)
+        old_last = rows_of(old_bank, "old_last", "old_last", nc.scalar.copy)
 
         kept = {}
 
@@ -94,18 +94,21 @@ def tile_picked_wema_tanh_lo_kernel(
         look_up(1, old_early, "kept1")
 
         w_dealt = w_raw[:].rearrange("p j (m t) -> p m j t", t=PACK)
-        w_first = keep.tile([P, P * PACK], BF16, name="w_first", tag="head", align_bytes=64)
-        w_rest = keep.tile([P, (PACK - 1) * P * PACK], BF16, name="w_rest", tag="rest", align_bytes=64)
-        w_codes = [keep.tile([P, P], U32, name="w_codes0", align_bytes=64), keep.tile([P, 3 * P], U32, name="w_codes1", align_bytes=64)]
-        w_plane = [keep.tile([P, P], U8, name="w_plane0", align_bytes=64), keep.tile([P, 3 * P], U8, name="w_plane1", align_bytes=64)]
-        nc.vector.tensor_copy(w_first[:].rearrange("p (m j) -> p m j", j=PACK), w_dealt[:, :, :, 0])
-        nc.scalar.copy(w_rest[:].rearrange("p (t m j) -> p m j t", t=PACK - 1, j=PACK), w_dealt[:, :, :, 1:PACK])
-        nc.vector.quantize_mx(w_codes[0][:].bitcast(FP8X4), w_plane[0][:], w_first[:])
+        w_codes, w_plane, w_pairs = [], [], []
+        for h, (tag, copy) in enumerate((("head", nc.vector.tensor_copy), ("rest", nc.scalar.copy))):
+            w_pairs.append(keep.tile([P, 2 * P * PACK], BF16, name=f"w_pairs{h}", tag=tag, align_bytes=64))
+            w_codes.append(keep.tile([P, 2 * P], U32, name=f"w_codes{h}", align_bytes=64))
+            w_plane.append(keep.tile([P, 2 * P], U8, name=f"w_plane{h}", align_bytes=64))
+            copy(w_pairs[h][:].rearrange("p (t m j) -> p m j t", t=2, j=PACK), w_dealt[:, :, :, 2 * h : 2 * h + 2])
+        for h in range(2):
+            nc.vector.quantize_mx(w_codes[h][:].bitcast(FP8X4), w_plane[h][:], w_pairs[h][:])
 
-        y = [keep.tile([P, T], F32, name=f"y{t}") for t in range(PACK)]
+        y_single = [keep.tile([P, T], F32, name=f"y{t}") for t in range(2)]
+        y_pair = keep.tile([P, 2, T], F32, name="y_pair")
+        y = [y_single[0][:], y_single[1][:], y_pair[:, 0, :], y_pair[:, 1, :]]
 
         def project(t):
-            part, cols = (0, slice(0, P)) if t == 0 else (1, slice((t - 1) * P, t * P))
+            part, cols = t // 2, slice((t % 2) * P, (t % 2 + 1) * P)
             acc = psum.tile([P, T], F32, name=f"acc{t}")
             nc.tensor.matmul_mx(
                 out=acc[:],
@@ -116,52 +119,52 @@ def tile_picked_wema_tanh_lo_kernel(
                 start=True,
                 stop=True,
             )
-            nc.scalar.activation(y[t][:], acc[:], TANH)
+            nc.scalar.activation(y[t], acc[:], TANH)
 
-        project(0)
-        look_up(2, old_late, "head")
-        nc.vector.quantize_mx(w_codes[1][:, 0:P].bitcast(FP8X4), w_plane[1][:, 0:P], w_rest[:, 0 : P * PACK])
-        nc.vector.quantize_mx(w_codes[1][:, P : 3 * P].bitcast(FP8X4), w_plane[1][:, P : 3 * P], w_rest[:, P * PACK : 3 * P * PACK])
-        for t in range(1, PACK):
+        for t in range(PACK):
             project(t)
-        look_up(3, old_late, "kept3")
+        look_up(2, old_late, "rest")
+        picked = keep.tile([P, T], F32, name="picked", tag="late", align_bytes=64)
+        nc.vector.tensor_copy(picked[:], window[3][:].indirect(offsets[:]))
 
-        grouped = [keep.tile([P, QUARTER, PACK], BF16, name=f"grouped{c}", align_bytes=64) for c in range(4)]
+        chunks = [slice(0, U // 2), slice(U // 2, 3 * U // 4), slice(3 * U // 4, U)]
+        grouped = [
+            keep.tile([P, cols.stop - cols.start, PACK], BF16, name=f"grouped{c}", align_bytes=64)
+            for c, cols in enumerate(chunks)
+        ]
         codes = keep.tile([P, U], U32, name="codes", align_bytes=64)
         plane = keep.tile([P, U], U8, name="plane", align_bytes=64)
 
-        def cols_of(c):
-            return slice(c * QUARTER, (c + 1) * QUARTER)
-
         for t in range(PACK):
-            engine = nc.vector if t == 0 else nc.gpsimd
-            fresh = keep.tile([P, T], F32, name="fresh", tag="blend", align_bytes=64)
             moved = keep.tile([P, T], F32, name=f"moved{t}")
-            engine.tensor_tensor(fresh[:], y[t][:], new_rows[:], MULT)
-            engine.tensor_tensor(moved[:], kept[t][:], fresh[:], ADD)
+            if t < 2:
+                single = keep.tile([P, T], F32, name=f"fresh{t}", tag="blend", align_bytes=64)
+                nc.gpsimd.tensor_tensor(single[:], y[t], new_rows[:], MULT)
+                fresh = single[:]
+            elif t == 2:
+                pair = keep.tile([P, 2, T], F32, name="fresh_pair", tag="blend", align_bytes=64)
+                nc.gpsimd.tensor_tensor(pair[:], y_pair[:], new_rows[:].unsqueeze(1).to_broadcast([P, 2, T]), MULT)
+                fresh = pair[:, 0, :]
+            else:
+                kept[t] = keep.tile([P, T], F32, name=f"kept{t}", tag="rest", align_bytes=64)
+                nc.gpsimd.tensor_tensor(kept[t][:], picked[:], old_last[:], MULT)
+                fresh = pair[:, 1, :]
+            (nc.vector if t == 0 else nc.gpsimd).tensor_tensor(moved[:], kept[t][:], fresh, ADD)
             nc.vector.tensor_copy(window[t][:].indirect(offsets[:]), moved[:])
             nc.sync.dma_start(out_rows[:, t, :], window[t][:])
             if t < PACK - 1:
-                for c in range(4):
-                    nc.scalar.copy(grouped[c][:, :, t], window[t][:, cols_of(c)])
-                    if t == PACK - 2 and c < 2:
-                        last = (c + 1) * QUARTER - 1
-                        nc.scalar.copy(
-                            grouped[c][:, QUARTER - 1, t : t + 2], window[t][:, last : last + 1].to_broadcast([P, 2])
-                        )
+                for c, cols in enumerate(chunks):
+                    nc.scalar.copy(grouped[c][:, :, t], window[t][:, cols])
+                    if t == PACK - 2 and c == 0:
+                        nc.scalar.copy(grouped[c][:, 0, t : t + 2], window[t][:, 0:1].to_broadcast([P, 2]))
 
-        t = PACK - 1
-        for c in range(4):
-            if c < 2:
-                nc.vector.tensor_copy(grouped[c][:, :, t], window[t][:, cols_of(c)])
-            else:
-                nc.scalar.copy(grouped[c][:, :, t], window[t][:, cols_of(c)])
         words = out_1[0].rearrange("p u j -> p (u j)").bitcast(I32)
-        for c in range(4):
-            nc.vector.quantize_mx(
-                codes[:, cols_of(c)].bitcast(FP8X4), plane[:, cols_of(c)], grouped[c][:].rearrange("p u j -> p (u j)")
-            )
-            nc.sync.dma_start(words[:, cols_of(c)], codes[:, cols_of(c)].bitcast(I32))
+        for c, cols in enumerate(chunks):
+            copy = nc.vector.tensor_copy if c == 0 else nc.scalar.copy
+            copy(grouped[c][:, :, PACK - 1], window[PACK - 1][:, cols])
+        for c, cols in enumerate(chunks):
+            nc.vector.quantize_mx(codes[:, cols].bitcast(FP8X4), plane[:, cols], grouped[c][:].rearrange("p u j -> p (u j)"))
+            nc.sync.dma_start(words[:, cols], codes[:, cols].bitcast(I32))
         for q in range(P // QUAD):
             queue = nc.scalar if q % 2 == 0 else nc.sync
             queue.dma_start(out_2[0, 4 * q : 4 * q + 4, :].bitcast(I32), plane[QUAD * q : QUAD * q + 4, :].bitcast(I32))

@@ -6,7 +6,9 @@ from concourse.masks import make_identity
 K, T, N, U = 512, 512, 512, 1024
 P = 128
 PACK = 4
-QUAD = 32
+QUADRANT = 32
+BLOCKS = T // P
+PAIR = 2
 
 F32 = mybir.dt.float32
 BF16 = mybir.dt.bfloat16
@@ -18,9 +20,20 @@ FP8X4 = mybir.dt.float8_e4m3fn_x4
 MULT = mybir.AluOpType.mult
 ADD = mybir.AluOpType.add
 TANH = mybir.ActivationFunctionType.Tanh
+COPY = mybir.ActivationFunctionType.Copy
+
+W_LOW = "w_low"
+W_HIGH = "w_high"
+KEPT = "kept"
+TANHS = "tanhs"
+FRESH = "fresh"
 
 FLOPS = 2 * K * N * T
 BYTES = K * T + K * T // 32 + 4 * N * U + 4 * K * N + 2 * 4 * T + 2 * P * T // 16 + 4 * N * U + N * U + N * U // 32
+
+
+def block(b):
+    return slice(b * P, (b + 1) * P)
 
 
 def tile_picked_wema_tanh_lo_kernel(
@@ -34,137 +47,161 @@ def tile_picked_wema_tanh_lo_kernel(
         keep = ctx.enter_context(tc.tile_pool(name="keep", bufs=1))
         psum = ctx.enter_context(tc.psum_pool(name="psum", bufs=1))
 
+        def shared(shape, dtype, name, tag):
+            return keep.tile(shape, dtype, name=name, tag=tag, align_bytes=64)
+
         offsets = keep.tile([P, T // 16], U16, name="offsets")
         window = [keep.tile([P, U], F32, name=f"window{t}") for t in range(PACK)]
         w_raw = keep.tile([P, PACK, N], F32, name="w_raw")
         x_codes = keep.tile([P, T], U32, name="x_codes", align_bytes=64)
         x_plane = keep.tile([P, T], U8, name="x_plane", align_bytes=64)
-        old_cols = keep.tile([P, PACK], F32, name="old_cols")
-        new_cols = keep.tile([P, PACK], F32, name="new_cols")
+        weight_blocks = keep.tile([P, P], F32, name="weight_blocks")
+        old_rows = keep.tile([P, T], F32, name="old_rows")
+        new_rows = keep.tile([P, T], F32, name="new_rows")
         identity = keep.tile([P, P], F32, name="identity")
-        warm_in = keep.tile([P, 1], F32, name="warm_in")
-        warm_out = keep.tile([P, 1], F32, name="warm_out")
 
-        nc.vector.memset(x_plane[:].bitcast(I32), 0)
-        nc.sync.dma_start(old_cols[:], old[0, :].rearrange("(p i) -> p i", i=PACK))
-        nc.scalar.dma_start(new_cols[:], new[0, :].rearrange("(p i) -> p i", i=PACK))
+        nc.gpsimd.memset(x_plane[:].bitcast(I32), 0)
+        for h, weights in enumerate((old, new)):
+            nc.sync.dma_start(
+                weight_blocks[h * P // 2 : (h + 1) * P // 2, :],
+                weights[0 : P // 2 // BLOCKS, :].rearrange("r (b q) -> (r b) q", b=BLOCKS),
+            )
         nc.sync.dma_start(window[0][:], mem_rows[:, 0, :])
         nc.sync.dma_start(offsets[:], slot)
-        nc.sync.dma_start(window[1][:], mem_rows[:, 1, :])
         nc.sync.dma_start(w_raw[:], w1.rearrange("(p j) n -> p j n", j=PACK))
-        nc.sync.dma_start(x_codes[:].bitcast(I32), x_words[0].rearrange("p n j -> p (n j)").bitcast(I32))
-        for q in range(P // QUAD):
+        for q in range(P // QUADRANT):
             nc.sync.dma_start(
-                x_plane[QUAD * q : QUAD * q + 4, :].bitcast(I32), x_scales[0, 4 * q : 4 * q + 4, :].bitcast(I32)
+                x_plane[QUADRANT * q : QUADRANT * q + 4, :].bitcast(I32), x_scales[0, 4 * q : 4 * q + 4, :].bitcast(I32)
             )
-        for t in range(2, PACK):
+        nc.sync.dma_start(x_codes[:].bitcast(I32), x_words[0].rearrange("p n j -> p (n j)").bitcast(I32))
+        for t in range(1, PACK):
             nc.sync.dma_start(window[t][:], mem_rows[:, t, :])
+        nc.sync.dma_start(old_rows[:], old)
+        nc.sync.dma_start(new_rows[:], new)
 
-        nc.vector.memset(warm_in[:], 0.0)
-        nc.scalar.activation(warm_out[:], warm_in[:], TANH)
+        zero = keep.tile([P, 1], F32, name="zero")
+        no_bias = keep.tile([P, 1], F32, name="no_bias")
+        nc.vector.memset(zero[:], 0.0)
+        nc.scalar.activation(no_bias[:], zero[:], TANH)
 
         make_identity(nc, identity[:])
+        weight_bank = psum.tile([P, 2, P // 2], F32, name="weight_bank", tag="turn", bufs=2)
+        nc.tensor.transpose(weight_bank[:].rearrange("p h r -> p (h r)"), weight_blocks[:], identity[:])
+        weight_cols = keep.tile([P, 2, BLOCKS], F32, name="weight_cols")
+        nc.scalar.copy(weight_cols[:], weight_bank[:, :, 0:BLOCKS])
 
-        def spread(cols, label):
-            bank = psum.tile([P, PACK, P], F32, name=f"{label}_bank")
-            for i in range(PACK):
-                nc.tensor.transpose(bank[:, i, :], cols[:, i : i + 1].to_broadcast([P, P]), identity[:])
-            return bank
+        def gather(t, picked):
+            nc.vector.tensor_copy(picked, window[t][:].indirect(offsets[:]))
 
-        def rows_of(bank, label, tag, copy):
-            rows = keep.tile([P, T], F32, name=label, tag=tag, align_bytes=64)
-            copy(rows[:].rearrange("p (n i) -> p n i", i=PACK), bank[:].rearrange("p i n -> p n i"))
-            return rows
+        def times_old_turned(t, picked):
+            bank = psum.tile([P, BLOCKS, P], F32, name=f"picked_bank{t}", tag="turn", bufs=2)
+            for b in range(BLOCKS):
+                nc.tensor.transpose(bank[:, b, :], picked[:, block(b)], identity[:])
+            kept = shared([P, BLOCKS, P], F32, f"kept{t}", KEPT)
+            for b in range(BLOCKS):
+                nc.scalar.activation(kept[:, b, :], bank[:, b, :], COPY, scale=weight_cols[:, 0, b : b + 1])
+            return kept
 
-        old_bank = spread(old_cols, "old")
-        new_bank = spread(new_cols, "new")
-        old_first = rows_of(old_bank, "old_first", "rest", nc.vector.tensor_copy)
-        old_early = rows_of(old_bank, "old_early", "head", nc.scalar.copy)
-        old_late = rows_of(old_bank, "old_late", "late", nc.scalar.copy)
-        new_rows = rows_of(new_bank, "new_rows", "new_rows", nc.scalar.copy)
-        old_last = rows_of(old_bank, "old_last", "old_last", nc.scalar.copy)
-
-        kept = {}
-
-        def look_up(t, old_rows, tag):
-            kept[t] = keep.tile([P, T], F32, name=f"kept{t}", tag=tag, align_bytes=64)
-            nc.vector.tensor_tensor(kept[t][:], window[t][:].indirect(offsets[:]), old_rows[:], MULT)
-
-        look_up(0, old_first, "kept0")
-        look_up(1, old_early, "kept1")
+        picked0 = shared([P, T], F32, "picked0", W_HIGH)
+        gather(0, picked0[:])
+        kept0 = times_old_turned(0, picked0)
 
         w_dealt = w_raw[:].rearrange("p j (m t) -> p m j t", t=PACK)
-        w_codes, w_plane, w_pairs = [], [], []
-        for h, (tag, copy) in enumerate((("head", nc.vector.tensor_copy), ("rest", nc.scalar.copy))):
-            w_pairs.append(keep.tile([P, 2 * P * PACK], BF16, name=f"w_pairs{h}", tag=tag, align_bytes=64))
-            w_codes.append(keep.tile([P, 2 * P], U32, name=f"w_codes{h}", align_bytes=64))
-            w_plane.append(keep.tile([P, 2 * P], U8, name=f"w_plane{h}", align_bytes=64))
-            copy(w_pairs[h][:].rearrange("p (t m j) -> p m j t", t=2, j=PACK), w_dealt[:, :, :, 2 * h : 2 * h + 2])
+        w_codes = keep.tile([P, N], U32, name="w_codes", align_bytes=64)
+        w_plane = keep.tile([P, N], U8, name="w_plane", align_bytes=64)
+        w_rounded = []
+        for h, (tag, copy) in enumerate(((W_LOW, nc.vector.tensor_copy), (W_HIGH, nc.scalar.copy))):
+            w_rounded.append(shared([P, PAIR * P * PACK], BF16, f"w_rounded{h}", tag))
+            copy(
+                w_rounded[h][:].rearrange("p (t m j) -> p m j t", t=PAIR, j=PACK),
+                w_dealt[:, :, :, PAIR * h : PAIR * (h + 1)],
+            )
         for h in range(2):
-            nc.vector.quantize_mx(w_codes[h][:].bitcast(FP8X4), w_plane[h][:], w_pairs[h][:])
+            cols = slice(h * PAIR * P, (h + 1) * PAIR * P)
+            nc.vector.quantize_mx(w_codes[:, cols].bitcast(FP8X4), w_plane[:, cols], w_rounded[h][:])
 
-        y_single = [keep.tile([P, T], F32, name=f"y{t}") for t in range(2)]
-        y_pair = keep.tile([P, 2, T], F32, name="y_pair")
-        y = [y_single[0][:], y_single[1][:], y_pair[:, 0, :], y_pair[:, 1, :]]
+        picked1 = shared([P, T], F32, "picked1", W_LOW)
+        gather(1, picked1[:])
+        picked_pair = shared([P, PAIR, T], F32, "picked_pair", W_HIGH)
+        for i in range(PAIR):
+            gather(PAIR + i, picked_pair[:, i, :])
 
-        def project(t):
-            part, cols = t // 2, slice((t % 2) * P, (t % 2 + 1) * P)
-            acc = psum.tile([P, T], F32, name=f"acc{t}")
+        moved = [keep.tile([P, T], F32, name=f"moved{t}") for t in range(PACK)]
+
+        def blend_turned(t, kept):
+            acc = psum.tile([P, BLOCKS, P], F32, name=f"acc{t}", tag="acc", bufs=2)
+            for b in range(BLOCKS):
+                nc.tensor.matmul_mx(
+                    out=acc[:, b, :],
+                    lhsT=x_codes[:, block(b)].bitcast(FP8X4),
+                    lhsT_scale=x_plane[:, block(b)],
+                    rhs=w_codes[:, block(t)].bitcast(FP8X4),
+                    rhs_scale=w_plane[:, block(t)],
+                    start=True,
+                    stop=True,
+                )
+            y = shared([P, BLOCKS, P], F32, f"y{t}", TANHS)
+            nc.scalar.activation(y[:], acc[:], TANH, bias=no_bias[:])
+            fresh = shared([P, BLOCKS, P], F32, f"fresh{t}", FRESH)
+            for b in range(BLOCKS):
+                nc.scalar.activation(fresh[:, b, :], y[:, b, :], COPY, scale=weight_cols[:, 1, b : b + 1])
+            bank = psum.tile([P, T], F32, name=f"sum_bank{t}")
+            for b in range(BLOCKS):
+                for term, first in ((kept, True), (fresh, False)):
+                    nc.tensor.matmul(
+                        bank[:, block(b)], term[:, b, :], identity[:], start=first, stop=not first, is_transpose=True
+                    )
+            nc.scalar.copy(moved[t][:], bank[:])
+
+        blend_turned(0, kept0)
+        blend_turned(1, times_old_turned(1, picked1))
+
+        y_pair = shared([P, PAIR, T], F32, "y_pair", TANHS)
+        for i in range(PAIR):
+            acc = psum.tile([P, T], F32, name=f"acc{PAIR + i}")
             nc.tensor.matmul_mx(
                 out=acc[:],
-                lhsT=w_codes[part][:, cols].bitcast(FP8X4),
-                lhsT_scale=w_plane[part][:, cols],
+                lhsT=w_codes[:, block(PAIR + i)].bitcast(FP8X4),
+                lhsT_scale=w_plane[:, block(PAIR + i)],
                 rhs=x_codes[:].bitcast(FP8X4),
                 rhs_scale=x_plane[:],
                 start=True,
                 stop=True,
             )
-            nc.scalar.activation(y[t], acc[:], TANH)
+            nc.scalar.activation(y_pair[:, i, :], acc[:], TANH, bias=no_bias[:])
+        kept_pair = keep.tile([P, PAIR, T], F32, name="kept_pair")
+        nc.gpsimd.tensor_tensor(kept_pair[:], picked_pair[:], old_rows[:].unsqueeze(1).to_broadcast([P, PAIR, T]), MULT)
+        fresh_pair = shared([P, PAIR, T], F32, "fresh_pair", W_HIGH)
+        nc.gpsimd.tensor_tensor(fresh_pair[:], y_pair[:], new_rows[:].unsqueeze(1).to_broadcast([P, PAIR, T]), MULT)
+        for i in range(PAIR):
+            nc.gpsimd.tensor_tensor(moved[PAIR + i][:], kept_pair[:, i, :], fresh_pair[:, i, :], ADD)
 
+        rounded = shared([P, U, PACK], BF16, "rounded", FRESH)
+        half = U // 2
         for t in range(PACK):
-            project(t)
-        look_up(2, old_late, "rest")
-        picked = keep.tile([P, T], F32, name="picked", tag="late", align_bytes=64)
-        nc.vector.tensor_copy(picked[:], window[3][:].indirect(offsets[:]))
-
-        chunks = [slice(0, U // 2), slice(U // 2, 3 * U // 4), slice(3 * U // 4, U)]
-        grouped = [
-            keep.tile([P, cols.stop - cols.start, PACK], BF16, name=f"grouped{c}", align_bytes=64)
-            for c, cols in enumerate(chunks)
-        ]
-        codes = keep.tile([P, U], U32, name="codes", align_bytes=64)
-        plane = keep.tile([P, U], U8, name="plane", align_bytes=64)
-
-        for t in range(PACK):
-            moved = keep.tile([P, T], F32, name=f"moved{t}")
-            if t < 2:
-                single = keep.tile([P, T], F32, name=f"fresh{t}", tag="blend", align_bytes=64)
-                nc.gpsimd.tensor_tensor(single[:], y[t], new_rows[:], MULT)
-                fresh = single[:]
-            elif t == 2:
-                pair = keep.tile([P, 2, T], F32, name="fresh_pair", tag="blend", align_bytes=64)
-                nc.gpsimd.tensor_tensor(pair[:], y_pair[:], new_rows[:].unsqueeze(1).to_broadcast([P, 2, T]), MULT)
-                fresh = pair[:, 0, :]
-            else:
-                kept[t] = keep.tile([P, T], F32, name=f"kept{t}", tag="rest", align_bytes=64)
-                nc.gpsimd.tensor_tensor(kept[t][:], picked[:], old_last[:], MULT)
-                fresh = pair[:, 1, :]
-            (nc.vector if t == 0 else nc.gpsimd).tensor_tensor(moved[:], kept[t][:], fresh, ADD)
-            nc.vector.tensor_copy(window[t][:].indirect(offsets[:]), moved[:])
+            nc.vector.tensor_copy(window[t][:].indirect(offsets[:]), moved[t][:])
             nc.sync.dma_start(out_rows[:, t, :], window[t][:])
-            if t < PACK - 1:
-                for c, cols in enumerate(chunks):
-                    nc.scalar.copy(grouped[c][:, :, t], window[t][:, cols])
-                    if t == PACK - 2 and c == 0:
-                        nc.scalar.copy(grouped[c][:, 0, t : t + 2], window[t][:, 0:1].to_broadcast([P, 2]))
+            if t < PACK - 2:
+                nc.scalar.copy(rounded[:, :, t], window[t][:])
+            elif t == PACK - 2:
+                nc.scalar.copy(rounded[:, 0:half, t], window[t][:, 0:half])
+                nc.scalar.copy(rounded[:, 0, t : t + 2], window[t][:, 0:1].to_broadcast([P, 2]))
+                nc.scalar.copy(rounded[:, half:U, t], window[t][:, half:U])
 
-        words = out_1[0].rearrange("p u j -> p (u j)").bitcast(I32)
+        chunks = [slice(0, half), slice(half, 3 * U // 4), slice(3 * U // 4, U)]
         for c, cols in enumerate(chunks):
             copy = nc.vector.tensor_copy if c == 0 else nc.scalar.copy
-            copy(grouped[c][:, :, PACK - 1], window[PACK - 1][:, cols])
-        for c, cols in enumerate(chunks):
-            nc.vector.quantize_mx(codes[:, cols].bitcast(FP8X4), plane[:, cols], grouped[c][:].rearrange("p u j -> p (u j)"))
+            copy(rounded[:, cols, PACK - 1], window[PACK - 1][:, cols])
+        codes = keep.tile([P, U], U32, name="codes", align_bytes=64)
+        plane = keep.tile([P, U], U8, name="plane", align_bytes=64)
+        words = out_1[0].rearrange("p u j -> p (u j)").bitcast(I32)
+        for cols in chunks:
+            nc.vector.quantize_mx(
+                codes[:, cols].bitcast(FP8X4), plane[:, cols], rounded[:, cols, :].rearrange("p u j -> p (u j)")
+            )
             nc.sync.dma_start(words[:, cols], codes[:, cols].bitcast(I32))
-        for q in range(P // QUAD):
+        for q in range(P // QUADRANT):
             queue = nc.scalar if q % 2 == 0 else nc.sync
-            queue.dma_start(out_2[0, 4 * q : 4 * q + 4, :].bitcast(I32), plane[QUAD * q : QUAD * q + 4, :].bitcast(I32))
+            queue.dma_start(
+                out_2[0, 4 * q : 4 * q + 4, :].bitcast(I32), plane[QUADRANT * q : QUADRANT * q + 4, :].bitcast(I32)
+            )

@@ -52,7 +52,7 @@ def tile_picked_wema_tanh_lo_kernel(
 
         offsets = keep.tile([P, T // 16], U16, name="offsets")
         window = [keep.tile([P, U], F32, name=f"window{t}") for t in range(PACK)]
-        w_raw = keep.tile([P, PACK, N], F32, name="w_raw")
+        w_raw = [keep.tile([P, PAIR, N], F32, name=f"w_raw{h}") for h in range(2)]
         x_codes = keep.tile([P, T], U32, name="x_codes", align_bytes=64)
         x_plane = keep.tile([P, T], U8, name="x_plane", align_bytes=64)
         weight_blocks = keep.tile([P, P], F32, name="weight_blocks")
@@ -61,14 +61,16 @@ def tile_picked_wema_tanh_lo_kernel(
         identity = keep.tile([P, P], F32, name="identity")
 
         nc.gpsimd.memset(x_plane[:].bitcast(I32), 0)
+        nc.sync.dma_start(window[0][:], mem_rows[:, 0, :])
+        nc.sync.dma_start(offsets[:], slot)
         for h, weights in enumerate((old, new)):
             nc.sync.dma_start(
                 weight_blocks[h * P // 2 : (h + 1) * P // 2, :],
                 weights[0 : P // 2 // BLOCKS, :].rearrange("r (b q) -> (r b) q", b=BLOCKS),
             )
-        nc.sync.dma_start(window[0][:], mem_rows[:, 0, :])
-        nc.sync.dma_start(offsets[:], slot)
-        nc.sync.dma_start(w_raw[:], w1.rearrange("(p j) n -> p j n", j=PACK))
+        w_rows = w1.rearrange("(p j) n -> p j n", j=PACK)
+        for h in range(2):
+            nc.sync.dma_start(w_raw[h][:], w_rows[:, PAIR * h : PAIR * (h + 1), :])
         for q in range(P // QUADRANT):
             nc.sync.dma_start(
                 x_plane[QUADRANT * q : QUADRANT * q + 4, :].bitcast(I32), x_scales[0, 4 * q : 4 * q + 4, :].bitcast(I32)
@@ -102,23 +104,26 @@ def tile_picked_wema_tanh_lo_kernel(
                 nc.scalar.activation(kept[:, b, :], bank[:, b, :], COPY, scale=weight_cols[:, 0, b : b + 1])
             return kept
 
-        picked0 = shared([P, T], F32, "picked0", W_HIGH)
+        picked0 = keep.tile([P, T], F32, name="picked0")
         gather(0, picked0[:])
         kept0 = times_old_turned(0, picked0)
 
-        w_dealt = w_raw[:].rearrange("p j (m t) -> p m j t", t=PACK)
         w_codes = keep.tile([P, N], U32, name="w_codes", align_bytes=64)
         w_plane = keep.tile([P, N], U8, name="w_plane", align_bytes=64)
-        w_rounded = []
-        for h, (tag, copy) in enumerate(((W_LOW, nc.vector.tensor_copy), (W_HIGH, nc.scalar.copy))):
-            w_rounded.append(shared([P, PAIR * P * PACK], BF16, f"w_rounded{h}", tag))
-            copy(
-                w_rounded[h][:].rearrange("p (t m j) -> p m j t", t=PAIR, j=PACK),
-                w_dealt[:, :, :, PAIR * h : PAIR * (h + 1)],
-            )
+        w_rounded = shared([P, N * PACK], BF16, "w_rounded", W_LOW)
+        w_places = w_rounded[:].rearrange("p (t m j) -> p m j t", t=PACK, j=PACK)
+        w_dealt = [w_raw[h][:].rearrange("p j (m t) -> p m j t", t=PACK) for h in range(2)]
+        nc.vector.tensor_copy(w_places[:, :, 0:PAIR, :], w_dealt[0])
+        for h in range(2):
+            pair = slice(PAIR * h, PAIR * (h + 1))
+            nc.vector.tensor_copy(w_places[:, :, PAIR:PACK, pair], w_dealt[1][:, :, :, pair])
         for h in range(2):
             cols = slice(h * PAIR * P, (h + 1) * PAIR * P)
-            nc.vector.quantize_mx(w_codes[:, cols].bitcast(FP8X4), w_plane[:, cols], w_rounded[h][:])
+            nc.vector.quantize_mx(
+                w_codes[:, cols].bitcast(FP8X4),
+                w_plane[:, cols],
+                w_rounded[:, h * PAIR * P * PACK : (h + 1) * PAIR * P * PACK],
+            )
 
         picked1 = shared([P, T], F32, "picked1", W_LOW)
         gather(1, picked1[:])
@@ -126,7 +131,7 @@ def tile_picked_wema_tanh_lo_kernel(
         for i in range(PAIR):
             gather(PAIR + i, picked_pair[:, i, :])
 
-        moved = [keep.tile([P, T], F32, name=f"moved{t}") for t in range(PACK)]
+        moved = [keep.tile([P, T], F32, name=f"moved{t}") for t in range(PAIR)]
 
         def blend_turned(t, kept):
             acc = psum.tile([P, BLOCKS, P], F32, name=f"acc{t}", tag="acc", bufs=2)
@@ -173,32 +178,45 @@ def tile_picked_wema_tanh_lo_kernel(
         nc.gpsimd.tensor_tensor(kept_pair[:], picked_pair[:], old_rows[:].unsqueeze(1).to_broadcast([P, PAIR, T]), MULT)
         fresh_pair = shared([P, PAIR, T], F32, "fresh_pair", W_HIGH)
         nc.gpsimd.tensor_tensor(fresh_pair[:], y_pair[:], new_rows[:].unsqueeze(1).to_broadcast([P, PAIR, T]), MULT)
-        for i in range(PAIR):
-            nc.gpsimd.tensor_tensor(moved[PAIR + i][:], kept_pair[:, i, :], fresh_pair[:, i, :], ADD)
 
         rounded = shared([P, U, PACK], BF16, "rounded", FRESH)
-        half = U // 2
+        quarter = U // 4
+        split = 9 * U // 16
         for t in range(PACK):
-            nc.vector.tensor_copy(window[t][:].indirect(offsets[:]), moved[t][:])
+            if t < PAIR:
+                nc.vector.tensor_copy(window[t][:].indirect(offsets[:]), moved[t][:])
+            else:
+                nc.vector.tensor_tensor(
+                    window[t][:].indirect(offsets[:]), kept_pair[:, t - PAIR, :], fresh_pair[:, t - PAIR, :], ADD
+                )
             nc.sync.dma_start(out_rows[:, t, :], window[t][:])
             if t < PACK - 2:
                 nc.scalar.copy(rounded[:, :, t], window[t][:])
             elif t == PACK - 2:
-                nc.scalar.copy(rounded[:, 0:half, t], window[t][:, 0:half])
-                nc.scalar.copy(rounded[:, 0, t : t + 2], window[t][:, 0:1].to_broadcast([P, 2]))
-                nc.scalar.copy(rounded[:, half:U, t], window[t][:, half:U])
+                nc.scalar.copy(rounded[:, 0:split, t], window[t][:, 0:split])
+                firsts = slice(0, quarter + 1, quarter)
+                nc.scalar.copy(
+                    rounded[:, firsts, t : t + 2], window[t][:, firsts].unsqueeze(2).to_broadcast([P, 2, 2])
+                )
+                nc.scalar.copy(rounded[:, split:U, t], window[t][:, split:U])
 
-        chunks = [slice(0, half), slice(half, 3 * U // 4), slice(3 * U // 4, U)]
-        for c, cols in enumerate(chunks):
-            copy = nc.vector.tensor_copy if c == 0 else nc.scalar.copy
+        chunks = [slice(0, U // 2), slice(U // 2, 3 * U // 4), slice(3 * U // 4, U)]
+        for copy, cols in (
+            (nc.vector.tensor_copy, slice(0, quarter)),
+            (nc.vector.tensor_copy, slice(quarter, split)),
+            (nc.scalar.copy, slice(split, 3 * U // 4)),
+            (nc.scalar.copy, slice(3 * U // 4, U)),
+        ):
             copy(rounded[:, cols, PACK - 1], window[PACK - 1][:, cols])
         codes = keep.tile([P, U], U32, name="codes", align_bytes=64)
         plane = keep.tile([P, U], U8, name="plane", align_bytes=64)
         words = out_1[0].rearrange("p u j -> p (u j)").bitcast(I32)
-        for cols in chunks:
+        for c in range(U // quarter):
+            cols = slice(c * quarter, (c + 1) * quarter)
             nc.vector.quantize_mx(
                 codes[:, cols].bitcast(FP8X4), plane[:, cols], rounded[:, cols, :].rearrange("p u j -> p (u j)")
             )
+        for cols in chunks:
             nc.sync.dma_start(words[:, cols], codes[:, cols].bitcast(I32))
         for q in range(P // QUADRANT):
             queue = nc.scalar if q % 2 == 0 else nc.sync

@@ -22,9 +22,8 @@ ADD = mybir.AluOpType.add
 TANH = mybir.ActivationFunctionType.Tanh
 COPY = mybir.ActivationFunctionType.Copy
 
-W_LOW = "w_low"
-W_HIGH = "w_high"
-KEPT = "kept"
+BIAS = "bias"
+FIRST = "first"
 TANHS = "tanhs"
 FRESH = "fresh"
 
@@ -56,18 +55,15 @@ def tile_picked_wema_tanh_lo_kernel(
         x_codes = keep.tile([P, T], U32, name="x_codes", align_bytes=64)
         x_plane = keep.tile([P, T], U8, name="x_plane", align_bytes=64)
         weight_blocks = keep.tile([P, P], F32, name="weight_blocks")
-        old_rows = keep.tile([P, T], F32, name="old_rows")
+        old_rows = shared([P, T], F32, "old_rows", FIRST)
         new_rows = keep.tile([P, T], F32, name="new_rows")
         identity = keep.tile([P, P], F32, name="identity")
 
         nc.gpsimd.memset(x_plane[:].bitcast(I32), 0)
-        nc.sync.dma_start(window[0][:], mem_rows[:, 0, :])
+        old_cols = keep.tile([P, PACK], F32, name="old_cols")
+        nc.sync.dma_start(old_cols[:], old[0, :].rearrange("(q i) -> q i", i=PACK))
+        nc.sync.dma_start(weight_blocks[:], new[0 : P // BLOCKS, :].rearrange("r (b q) -> (r b) q", b=BLOCKS))
         nc.sync.dma_start(offsets[:], slot)
-        for h, weights in enumerate((old, new)):
-            nc.sync.dma_start(
-                weight_blocks[h * P // 2 : (h + 1) * P // 2, :],
-                weights[0 : P // 2 // BLOCKS, :].rearrange("r (b q) -> (r b) q", b=BLOCKS),
-            )
         w_rows = w1.rearrange("(p j) n -> p j n", j=PACK)
         for h in range(2):
             nc.sync.dma_start(w_raw[h][:], w_rows[:, PAIR * h : PAIR * (h + 1), :])
@@ -76,47 +72,47 @@ def tile_picked_wema_tanh_lo_kernel(
                 x_plane[QUADRANT * q : QUADRANT * q + 4, :].bitcast(I32), x_scales[0, 4 * q : 4 * q + 4, :].bitcast(I32)
             )
         nc.sync.dma_start(x_codes[:].bitcast(I32), x_words[0].rearrange("p n j -> p (n j)").bitcast(I32))
-        for t in range(1, PACK):
+        for t in range(PACK):
             nc.sync.dma_start(window[t][:], mem_rows[:, t, :])
-        nc.sync.dma_start(old_rows[:], old)
         nc.sync.dma_start(new_rows[:], new)
 
         zero = keep.tile([P, 1], F32, name="zero")
-        no_bias = keep.tile([P, 1], F32, name="no_bias")
+        no_bias = shared([P, 1], F32, "no_bias", BIAS)
         nc.vector.memset(zero[:], 0.0)
         nc.scalar.activation(no_bias[:], zero[:], TANH)
 
         make_identity(nc, identity[:])
-        weight_bank = psum.tile([P, 2, P // 2], F32, name="weight_bank", tag="turn", bufs=2)
-        nc.tensor.transpose(weight_bank[:].rearrange("p h r -> p (h r)"), weight_blocks[:], identity[:])
-        weight_cols = keep.tile([P, 2, BLOCKS], F32, name="weight_cols")
-        nc.scalar.copy(weight_cols[:], weight_bank[:, :, 0:BLOCKS])
 
-        def gather(t, picked):
-            nc.vector.tensor_copy(picked, window[t][:].indirect(offsets[:]))
+        old_bank = psum.tile([P, PACK, P], F32, name="old_bank", tag="turn", bufs=2)
+        for i in range(PACK):
+            nc.tensor.transpose(old_bank[:, i, :], old_cols[:, i : i + 1].to_broadcast([P, P]), identity[:])
+        nc.scalar.copy(old_rows[:].rearrange("p (q i) -> p q i", i=PACK), old_bank[:].rearrange("p i q -> p q i"))
+
+        weight_bank = psum.tile([P, P], F32, name="weight_bank", tag="turn", bufs=2)
+        nc.tensor.transpose(weight_bank[:], weight_blocks[:], identity[:])
+        new_cols = keep.tile([P, BLOCKS], F32, name="new_cols")
+        nc.scalar.copy(new_cols[:], weight_bank[:, 0:BLOCKS])
+
+        def gather_times_old(t, kept):
+            nc.vector.tensor_tensor(kept, window[t][:].indirect(offsets[:]), old_rows[:], MULT)
 
         def times_old_turned(t, picked):
             bank = psum.tile([P, BLOCKS, P], F32, name=f"picked_bank{t}", tag="turn", bufs=2)
             for b in range(BLOCKS):
                 nc.tensor.transpose(bank[:, b, :], picked[:, block(b)], identity[:])
-            kept = shared([P, BLOCKS, P], F32, f"kept{t}", KEPT)
-            for b in range(BLOCKS):
-                nc.scalar.activation(kept[:, b, :], bank[:, b, :], COPY, scale=weight_cols[:, 0, b : b + 1])
+            kept = shared([P, BLOCKS, P], F32, f"kept{t}", FRESH)
+            nc.scalar.copy(kept[:], bank[:])
             return kept
-
-        picked0 = keep.tile([P, T], F32, name="picked0")
-        gather(0, picked0[:])
-        kept0 = times_old_turned(0, picked0)
 
         w_codes = keep.tile([P, N], U32, name="w_codes", align_bytes=64)
         w_plane = keep.tile([P, N], U8, name="w_plane", align_bytes=64)
-        w_rounded = shared([P, N * PACK], BF16, "w_rounded", W_LOW)
+        w_rounded = keep.tile([P, N * PACK], BF16, name="w_rounded", align_bytes=64)
         w_places = w_rounded[:].rearrange("p (t m j) -> p m j t", t=PACK, j=PACK)
         w_dealt = [w_raw[h][:].rearrange("p j (m t) -> p m j t", t=PACK) for h in range(2)]
         nc.vector.tensor_copy(w_places[:, :, 0:PAIR, :], w_dealt[0])
-        for h in range(2):
+        for h, copy in enumerate((nc.vector.tensor_copy, nc.scalar.copy)):
             pair = slice(PAIR * h, PAIR * (h + 1))
-            nc.vector.tensor_copy(w_places[:, :, PAIR:PACK, pair], w_dealt[1][:, :, :, pair])
+            copy(w_places[:, :, PAIR:PACK, pair], w_dealt[1][:, :, :, pair])
         for h in range(2):
             cols = slice(h * PAIR * P, (h + 1) * PAIR * P)
             nc.vector.quantize_mx(
@@ -125,19 +121,22 @@ def tile_picked_wema_tanh_lo_kernel(
                 w_rounded[:, h * PAIR * P * PACK : (h + 1) * PAIR * P * PACK],
             )
 
-        picked1 = shared([P, T], F32, "picked1", W_LOW)
-        gather(1, picked1[:])
-        picked_pair = shared([P, PAIR, T], F32, "picked_pair", W_HIGH)
+        kept0 = keep.tile([P, T], F32, name="kept_first")
+        gather_times_old(0, kept0[:])
+        picked1 = keep.tile([P, T], F32, name="picked1")
+        gather_times_old(1, picked1[:])
+        kept_pair = keep.tile([P, PAIR, T], F32, name="kept_pair")
         for i in range(PAIR):
-            gather(PAIR + i, picked_pair[:, i, :])
+            gather_times_old(PAIR + i, kept_pair[:, i, :])
 
-        moved = [keep.tile([P, T], F32, name=f"moved{t}") for t in range(PAIR)]
+        moved = [keep.tile([P, T], F32, name="fresh_first"), keep.tile([P, T], F32, name="moved1")]
 
-        def blend_turned(t, kept):
-            acc = psum.tile([P, BLOCKS, P], F32, name=f"acc{t}", tag="acc", bufs=2)
+        def blend_turned(t, kept, parts):
+            per = BLOCKS // parts
+            acc = [psum.tile([P, per, P], F32, name=f"acc{t}_{h}", tag=f"acc{t}_{h}") for h in range(parts)]
             for b in range(BLOCKS):
                 nc.tensor.matmul_mx(
-                    out=acc[:, b, :],
+                    out=acc[b // per][:, b % per, :],
                     lhsT=x_codes[:, block(b)].bitcast(FP8X4),
                     lhsT_scale=x_plane[:, block(b)],
                     rhs=w_codes[:, block(t)].bitcast(FP8X4),
@@ -146,24 +145,32 @@ def tile_picked_wema_tanh_lo_kernel(
                     stop=True,
                 )
             y = shared([P, BLOCKS, P], F32, f"y{t}", TANHS)
-            nc.scalar.activation(y[:], acc[:], TANH, bias=no_bias[:])
-            fresh = shared([P, BLOCKS, P], F32, f"fresh{t}", FRESH)
+            for h in range(parts):
+                nc.scalar.activation(y[:, h * per : (h + 1) * per, :], acc[h][:], TANH, bias=no_bias[:])
+            fresh = shared([P, BLOCKS, P], F32, f"fresh{t}", FRESH if t == 0 else "fresh1")
             for b in range(BLOCKS):
-                nc.scalar.activation(fresh[:, b, :], y[:, b, :], COPY, scale=weight_cols[:, 1, b : b + 1])
-            bank = psum.tile([P, T], F32, name=f"sum_bank{t}")
+                nc.scalar.activation(fresh[:, b, :], y[:, b, :], COPY, scale=new_cols[:, b : b + 1])
+            bank = [psum.tile([P, per * P], F32, name=f"sum{t}_{h}", tag=f"sum{t}_{h}") for h in range(parts)]
             for b in range(BLOCKS):
-                for term, first in ((kept, True), (fresh, False)):
+                terms = [fresh] + kept
+                for i, term in enumerate(terms):
                     nc.tensor.matmul(
-                        bank[:, block(b)], term[:, b, :], identity[:], start=first, stop=not first, is_transpose=True
+                        bank[b // per][:, block(b % per)],
+                        term[:, b, :],
+                        identity[:],
+                        start=i == 0,
+                        stop=i == len(terms) - 1,
+                        is_transpose=True,
                     )
-            nc.scalar.copy(moved[t][:], bank[:])
+            for h in range(parts):
+                nc.scalar.copy(moved[t][:, h * per * P : (h + 1) * per * P], bank[h][:])
 
-        blend_turned(0, kept0)
-        blend_turned(1, times_old_turned(1, picked1))
+        blend_turned(0, [], 1)
+        blend_turned(1, [times_old_turned(1, picked1)], 1)
 
-        y_pair = shared([P, PAIR, T], F32, "y_pair", TANHS)
+        y_pair = keep.tile([P, PAIR, T], F32, name="y_pair")
         for i in range(PAIR):
-            acc = psum.tile([P, T], F32, name=f"acc{PAIR + i}")
+            acc = psum.tile([P, T], F32, name=f"acc{PAIR + i}", tag=("sum0_0", "sum1_0")[i])
             nc.tensor.matmul_mx(
                 out=acc[:],
                 lhsT=w_codes[:, block(PAIR + i)].bitcast(FP8X4),
@@ -174,16 +181,16 @@ def tile_picked_wema_tanh_lo_kernel(
                 stop=True,
             )
             nc.scalar.activation(y_pair[:, i, :], acc[:], TANH, bias=no_bias[:])
-        kept_pair = keep.tile([P, PAIR, T], F32, name="kept_pair")
-        nc.gpsimd.tensor_tensor(kept_pair[:], picked_pair[:], old_rows[:].unsqueeze(1).to_broadcast([P, PAIR, T]), MULT)
-        fresh_pair = shared([P, PAIR, T], F32, "fresh_pair", W_HIGH)
+        fresh_pair = shared([P, PAIR, T], F32, "fresh_pair", FIRST)
         nc.gpsimd.tensor_tensor(fresh_pair[:], y_pair[:], new_rows[:].unsqueeze(1).to_broadcast([P, PAIR, T]), MULT)
 
-        rounded = shared([P, U, PACK], BF16, "rounded", FRESH)
+        rounded = shared([P, U, PACK], BF16, "rounded", BIAS)
         quarter = U // 4
         split = 9 * U // 16
         for t in range(PACK):
-            if t < PAIR:
+            if t == 0:
+                nc.vector.tensor_tensor(window[t][:].indirect(offsets[:]), kept0[:], moved[t][:], ADD)
+            elif t == 1:
                 nc.vector.tensor_copy(window[t][:].indirect(offsets[:]), moved[t][:])
             else:
                 nc.vector.tensor_tensor(
@@ -193,10 +200,8 @@ def tile_picked_wema_tanh_lo_kernel(
             if t < PACK - 2:
                 nc.scalar.copy(rounded[:, :, t], window[t][:])
             elif t == PACK - 2:
-                nc.scalar.copy(rounded[:, 0:split, t], window[t][:, 0:split])
-                firsts = slice(0, quarter + 1, quarter)
                 nc.scalar.copy(
-                    rounded[:, firsts, t : t + 2], window[t][:, firsts].unsqueeze(2).to_broadcast([P, 2, 2])
+                    rounded[:, 0:split, t : t + 2], window[t][:, 0:split].unsqueeze(2).to_broadcast([P, split, 2])
                 )
                 nc.scalar.copy(rounded[:, split:U, t], window[t][:, split:U])
 

@@ -20,6 +20,7 @@ FP8X4 = mybir.dt.float8_e4m3fn_x4
 MULT = mybir.AluOpType.mult
 ADD = mybir.AluOpType.add
 TANH = mybir.ActivationFunctionType.Tanh
+IDENTITY = mybir.ActivationFunctionType.Identity
 COPY = mybir.ActivationFunctionType.Copy
 
 BIAS = "bias"
@@ -110,15 +111,15 @@ def tile_picked_wema_tanh_lo_kernel(
         w_places = w_rounded[:].rearrange("p (t m j) -> p m j t", t=PACK, j=PACK)
         w_dealt = [w_raw[h][:].rearrange("p j (m t) -> p m j t", t=PACK) for h in range(2)]
         nc.vector.tensor_copy(w_places[:, :, 0:PAIR, :], w_dealt[0])
-        for h, copy in enumerate((nc.vector.tensor_copy, nc.scalar.copy)):
-            pair = slice(PAIR * h, PAIR * (h + 1))
-            copy(w_places[:, :, PAIR:PACK, pair], w_dealt[1][:, :, :, pair])
-        for h in range(2):
-            cols = slice(h * PAIR * P, (h + 1) * PAIR * P)
+        groups = (slice(0, 1), slice(1, PAIR), slice(PAIR, PACK))
+        for copy, ts in zip((nc.vector.tensor_copy, nc.vector.tensor_copy, nc.scalar.copy), groups):
+            copy(w_places[:, :, PAIR:PACK, ts], w_dealt[1][:, :, :, ts])
+        for ts in groups:
+            cols = slice(ts.start * P, ts.stop * P)
             nc.vector.quantize_mx(
                 w_codes[:, cols].bitcast(FP8X4),
                 w_plane[:, cols],
-                w_rounded[:, h * PAIR * P * PACK : (h + 1) * PAIR * P * PACK],
+                w_rounded[:, ts.start * P * PACK : ts.stop * P * PACK],
             )
 
         kept0 = keep.tile([P, T], F32, name="kept_first")
@@ -163,14 +164,16 @@ def tile_picked_wema_tanh_lo_kernel(
                         is_transpose=True,
                     )
             for h in range(parts):
-                nc.scalar.copy(moved[t][:, h * per * P : (h + 1) * per * P], bank[h][:])
+                nc.scalar.activation(
+                    moved[t][:, h * per * P : (h + 1) * per * P], bank[h][:], IDENTITY, bias=no_bias[:]
+                )
 
         blend_turned(0, [], 1)
         blend_turned(1, [times_old_turned(1, picked1)], 1)
 
-        y_pair = keep.tile([P, PAIR, T], F32, name="y_pair")
+        y_pair = shared([P, PAIR, T], F32, "y_pair", TANHS)
         for i in range(PAIR):
-            acc = psum.tile([P, T], F32, name=f"acc{PAIR + i}", tag=("sum0_0", "sum1_0")[i])
+            acc = psum.tile([P, T], F32, name=f"acc{PAIR + i}", tag=("acc2", "acc1_0")[i])
             nc.tensor.matmul_mx(
                 out=acc[:],
                 lhsT=w_codes[:, block(PAIR + i)].bitcast(FP8X4),
@@ -186,7 +189,7 @@ def tile_picked_wema_tanh_lo_kernel(
 
         rounded = shared([P, U, PACK], BF16, "rounded", BIAS)
         quarter = U // 4
-        split = 9 * U // 16
+        split = U // 2
         for t in range(PACK):
             if t == 0:
                 nc.vector.tensor_tensor(window[t][:].indirect(offsets[:]), kept0[:], moved[t][:], ADD)
@@ -205,19 +208,22 @@ def tile_picked_wema_tanh_lo_kernel(
                 )
                 nc.scalar.copy(rounded[:, split:U, t], window[t][:, split:U])
 
-        chunks = [slice(0, U // 2), slice(U // 2, 3 * U // 4), slice(3 * U // 4, U)]
+        eighth = U // 8
+        chunks = [slice(0, split), slice(split, U - eighth), slice(U - eighth, U)]
         for copy, cols in (
             (nc.vector.tensor_copy, slice(0, quarter)),
             (nc.vector.tensor_copy, slice(quarter, split)),
             (nc.scalar.copy, slice(split, 3 * U // 4)),
-            (nc.scalar.copy, slice(3 * U // 4, U)),
+            (nc.scalar.copy, slice(3 * U // 4, U - eighth)),
+            (nc.scalar.copy, slice(U - eighth, U)),
         ):
             copy(rounded[:, cols, PACK - 1], window[PACK - 1][:, cols])
         codes = keep.tile([P, U], U32, name="codes", align_bytes=64)
         plane = keep.tile([P, U], U8, name="plane", align_bytes=64)
         words = out_1[0].rearrange("p u j -> p (u j)").bitcast(I32)
-        for c in range(U // quarter):
-            cols = slice(c * quarter, (c + 1) * quarter)
+        edges = [0, quarter, 2 * quarter, 3 * quarter, U - eighth, U]
+        for start, stop in zip(edges, edges[1:]):
+            cols = slice(start, stop)
             nc.vector.quantize_mx(
                 codes[:, cols].bitcast(FP8X4), plane[:, cols], rounded[:, cols, :].rearrange("p u j -> p (u j)")
             )

@@ -9,6 +9,7 @@ PACK = 4
 QUADRANT = 32
 BLOCKS = T // P
 PAIR = 2
+LEAD = 256
 
 F32 = mybir.dt.float32
 BF16 = mybir.dt.bfloat16
@@ -25,6 +26,7 @@ COPY = mybir.ActivationFunctionType.Copy
 
 BIAS = "bias"
 FIRST = "first"
+LEADING = "leading"
 TANHS = "tanhs"
 FRESH = "fresh"
 
@@ -45,6 +47,7 @@ def tile_picked_wema_tanh_lo_kernel(
 
     with ExitStack() as ctx:
         keep = ctx.enter_context(tc.tile_pool(name="keep", bufs=1))
+        reuse = ctx.enter_context(tc.tile_pool(name="reuse", bufs=1))
         psum = ctx.enter_context(tc.psum_pool(name="psum", bufs=1))
 
         def shared(shape, dtype, name, tag):
@@ -56,7 +59,7 @@ def tile_picked_wema_tanh_lo_kernel(
         x_codes = keep.tile([P, T], U32, name="x_codes", align_bytes=64)
         x_plane = keep.tile([P, T], U8, name="x_plane", align_bytes=64)
         weight_blocks = keep.tile([P, P], F32, name="weight_blocks")
-        old_rows = shared([P, T], F32, "old_rows", FIRST)
+        old_rows = reuse.tile([P, T], F32, name="old_rows", offset=0)
         new_rows = keep.tile([P, T], F32, name="new_rows")
         identity = keep.tile([P, P], F32, name="identity")
 
@@ -72,7 +75,8 @@ def tile_picked_wema_tanh_lo_kernel(
             nc.sync.dma_start(
                 x_plane[QUADRANT * q : QUADRANT * q + 4, :].bitcast(I32), x_scales[0, 4 * q : 4 * q + 4, :].bitcast(I32)
             )
-        nc.sync.dma_start(x_codes[:].bitcast(I32), x_words[0].rearrange("p n j -> p (n j)").bitcast(I32))
+        x_rows = x_words[0].rearrange("p n j -> p (n j)").bitcast(I32)
+        nc.sync.dma_start(x_codes[:].bitcast(I32), x_rows)
         for t in range(PACK):
             nc.sync.dma_start(window[t][:], mem_rows[:, t, :])
         nc.sync.dma_start(new_rows[:], new)
@@ -80,6 +84,12 @@ def tile_picked_wema_tanh_lo_kernel(
         zero = keep.tile([P, 1], F32, name="zero")
         no_bias = shared([P, 1], F32, "no_bias", BIAS)
         nc.vector.memset(zero[:], 0.0)
+        lead_bias = shared([P, 1], F32, "lead_bias", LEADING)
+        nc.vector.memset(lead_bias[:], 0.0)
+        unit = reuse.tile([P, 1], F32, name="unit", offset=4 * T)
+        nc.vector.memset(unit[:], 1.0)
+        rest_bias = shared([P, 1], F32, "rest_bias", "rest")
+        nc.vector.memset(rest_bias[:], 0.0)
         nc.scalar.activation(no_bias[:], zero[:], TANH)
 
         make_identity(nc, identity[:])
@@ -98,7 +108,7 @@ def tile_picked_wema_tanh_lo_kernel(
             nc.vector.tensor_tensor(kept, window[t][:].indirect(offsets[:]), old_rows[:], MULT)
 
         def times_old_turned(t, picked):
-            bank = psum.tile([P, BLOCKS, P], F32, name=f"picked_bank{t}", tag="turn", bufs=2)
+            bank = psum.tile([P, BLOCKS, P], F32, name=f"picked_bank{t}", tag="sum0a")
             for b in range(BLOCKS):
                 nc.tensor.transpose(bank[:, b, :], picked[:, block(b)], identity[:])
             kept = shared([P, BLOCKS, P], F32, f"kept{t}", FRESH)
@@ -122,22 +132,19 @@ def tile_picked_wema_tanh_lo_kernel(
                 w_rounded[:, ts.start * P * PACK : ts.stop * P * PACK],
             )
 
-        kept0 = keep.tile([P, T], F32, name="kept_first")
+        kept0 = keep.tile([P, T], F32, name="kept0")
         gather_times_old(0, kept0[:])
         picked1 = keep.tile([P, T], F32, name="picked1")
         gather_times_old(1, picked1[:])
-        kept_pair = keep.tile([P, PAIR, T], F32, name="kept_pair")
-        for i in range(PAIR):
-            gather_times_old(PAIR + i, kept_pair[:, i, :])
 
         moved = [keep.tile([P, T], F32, name="fresh_first"), keep.tile([P, T], F32, name="moved1")]
 
-        def blend_turned(t, kept, parts):
-            per = BLOCKS // parts
-            acc = [psum.tile([P, per, P], F32, name=f"acc{t}_{h}", tag=f"acc{t}_{h}") for h in range(parts)]
-            for b in range(BLOCKS):
+        def blend_turned(name, t, blocks, kept, fresh_tag, bias, scale=1.0):
+            count = len(blocks)
+            acc = psum.tile([P, count, P], F32, name=f"acc{name}", tag=f"acc{name}")
+            for i, b in enumerate(blocks):
                 nc.tensor.matmul_mx(
-                    out=acc[b // per][:, b % per, :],
+                    out=acc[:, i, :],
                     lhsT=x_codes[:, block(b)].bitcast(FP8X4),
                     lhsT_scale=x_plane[:, block(b)],
                     rhs=w_codes[:, block(t)].bitcast(FP8X4),
@@ -145,35 +152,43 @@ def tile_picked_wema_tanh_lo_kernel(
                     start=True,
                     stop=True,
                 )
-            y = shared([P, BLOCKS, P], F32, f"y{t}", TANHS)
-            for h in range(parts):
-                nc.scalar.activation(y[:, h * per : (h + 1) * per, :], acc[h][:], TANH, bias=no_bias[:])
-            fresh = shared([P, BLOCKS, P], F32, f"fresh{t}", FRESH if t == 0 else "fresh1")
-            for b in range(BLOCKS):
-                nc.scalar.activation(fresh[:, b, :], y[:, b, :], COPY, scale=new_cols[:, b : b + 1])
-            bank = [psum.tile([P, per * P], F32, name=f"sum{t}_{h}", tag=f"sum{t}_{h}") for h in range(parts)]
-            for b in range(BLOCKS):
-                terms = [fresh] + kept
-                for i, term in enumerate(terms):
+            y = shared([P, count, P], F32, f"y{name}", TANHS)
+            nc.scalar.activation(y[:], acc[:], TANH, bias=no_bias[:])
+            fresh = shared([P, count, P], F32, f"fresh{name}", fresh_tag)
+            for i, b in enumerate(blocks):
+                nc.scalar.activation(fresh[:, i, :], y[:, i, :], COPY, scale=new_cols[:, b : b + 1])
+            bank = psum.tile([P, count * P], F32, name=f"sum{name}", tag=f"sum{name}")
+            for i, b in enumerate(blocks):
+                terms = [fresh[:, i, :]] + [term[:, b, :] for term in kept]
+                for n, term in enumerate(terms):
                     nc.tensor.matmul(
-                        bank[b // per][:, block(b % per)],
-                        term[:, b, :],
+                        bank[:, block(i)],
+                        term,
                         identity[:],
-                        start=i == 0,
-                        stop=i == len(terms) - 1,
+                        start=n == 0,
+                        stop=n == len(terms) - 1,
                         is_transpose=True,
                     )
-            for h in range(parts):
-                nc.scalar.activation(
-                    moved[t][:, h * per * P : (h + 1) * per * P], bank[h][:], IDENTITY, bias=no_bias[:]
-                )
+            cols = slice(blocks[0] * P, (blocks[-1] + 1) * P)
+            nc.scalar.activation(moved[t][:, cols], bank[:], IDENTITY, bias=bias[:], scale=scale)
 
-        blend_turned(0, [], 1)
-        blend_turned(1, [times_old_turned(1, picked1)], 1)
+        def scatter_first(cols):
+            entries = offsets[:, cols.start // 16 : cols.stop // 16]
+            nc.vector.tensor_tensor(window[0][:].indirect(entries), kept0[:, cols], moved[0][:, cols], ADD)
+
+        blend_turned("0a", 0, list(range(LEAD // P)), [], "fresh0a", lead_bias)
+        scatter_first(slice(0, LEAD))
+        kept_late = [shared([P, T], F32, "kept2", LEADING)]
+        gather_times_old(2, kept_late[0][:])
+        blend_turned("0b", 0, list(range(LEAD // P, BLOCKS)), [], FRESH, rest_bias)
+        scatter_first(slice(LEAD, T))
+        kept_late.append(shared([P, T], F32, "kept3", "rest"))
+        gather_times_old(3, kept_late[1][:])
+        blend_turned("1", 1, list(range(BLOCKS)), [times_old_turned(1, picked1)], "fresh1", no_bias, unit[:])
 
         y_pair = shared([P, PAIR, T], F32, "y_pair", TANHS)
         for i in range(PAIR):
-            acc = psum.tile([P, T], F32, name=f"acc{PAIR + i}", tag=("acc2", "acc1_0")[i])
+            acc = psum.tile([P, T], F32, name=f"acc{PAIR + i}", tag=("sum0b", "acc1")[i])
             nc.tensor.matmul_mx(
                 out=acc[:],
                 lhsT=w_codes[:, block(PAIR + i)].bitcast(FP8X4),
@@ -184,20 +199,18 @@ def tile_picked_wema_tanh_lo_kernel(
                 stop=True,
             )
             nc.scalar.activation(y_pair[:, i, :], acc[:], TANH, bias=no_bias[:])
-        fresh_pair = shared([P, PAIR, T], F32, "fresh_pair", FIRST)
+        fresh_pair = reuse.tile([P, PAIR, T], F32, name="fresh_pair", offset=0)
         nc.gpsimd.tensor_tensor(fresh_pair[:], y_pair[:], new_rows[:].unsqueeze(1).to_broadcast([P, PAIR, T]), MULT)
 
         rounded = shared([P, U, PACK], BF16, "rounded", BIAS)
         quarter = U // 4
         split = U // 2
         for t in range(PACK):
-            if t == 0:
-                nc.vector.tensor_tensor(window[t][:].indirect(offsets[:]), kept0[:], moved[t][:], ADD)
-            elif t == 1:
+            if t == 1:
                 nc.vector.tensor_copy(window[t][:].indirect(offsets[:]), moved[t][:])
-            else:
+            elif t > 1:
                 nc.vector.tensor_tensor(
-                    window[t][:].indirect(offsets[:]), kept_pair[:, t - PAIR, :], fresh_pair[:, t - PAIR, :], ADD
+                    window[t][:].indirect(offsets[:]), kept_late[t - PAIR][:], fresh_pair[:, t - PAIR, :], ADD
                 )
             nc.sync.dma_start(out_rows[:, t, :], window[t][:])
             if t < PACK - 2:

@@ -55,7 +55,7 @@ def tile_picked_wema_tanh_lo_kernel(
 
         offsets = keep.tile([P, T // 16], U16, name="offsets")
         window = [keep.tile([P, U], F32, name=f"window{t}") for t in range(PACK)]
-        w_raw = [keep.tile([P, PAIR, N], F32, name=f"w_raw{h}") for h in range(2)]
+        w_raw = [shared([P, PAIR, N], F32, f"w_raw{h}", f"w_raw{h}") for h in range(2)]
         x_codes = keep.tile([P, T], U32, name="x_codes", align_bytes=64)
         x_plane = keep.tile([P, T], U8, name="x_plane", align_bytes=64)
         weight_blocks = keep.tile([P, P], F32, name="weight_blocks")
@@ -86,6 +86,10 @@ def tile_picked_wema_tanh_lo_kernel(
         nc.vector.memset(zero[:], 0.0)
         lead_bias = shared([P, 1], F32, "lead_bias", LEADING)
         nc.vector.memset(lead_bias[:], 0.0)
+        spread_bias = shared([P, 1], F32, "spread_bias", "spread")
+        nc.vector.memset(spread_bias[:], 0.0)
+        spread_unit = shared([P, 1], F32, "spread_unit", "w_plane")
+        nc.vector.memset(spread_unit[:], 1.0)
         unit = reuse.tile([P, 1], F32, name="unit", offset=4 * T)
         nc.vector.memset(unit[:], 1.0)
         rest_bias = shared([P, 1], F32, "rest_bias", "rest")
@@ -97,7 +101,15 @@ def tile_picked_wema_tanh_lo_kernel(
         old_bank = psum.tile([P, PACK, P], F32, name="old_bank", tag="turn", bufs=2)
         for i in range(PACK):
             nc.tensor.transpose(old_bank[:, i, :], old_cols[:, i : i + 1].to_broadcast([P, P]), identity[:])
-        nc.scalar.copy(old_rows[:].rearrange("p (q i) -> p q i", i=PACK), old_bank[:].rearrange("p i q -> p q i"))
+        nc.scalar.activation(
+            old_rows[:].rearrange("p (q i) -> p q i", i=PACK),
+            old_bank[:].rearrange("p i q -> p q i"),
+            IDENTITY,
+            bias=spread_bias[:],
+            scale=spread_unit[:],
+        )
+        round_unit = shared([P, 1], F32, "round_unit", "spread")
+        nc.scalar.copy(round_unit[:], unit[:])
 
         weight_bank = psum.tile([P, P], F32, name="weight_bank", tag="turn", bufs=2)
         nc.tensor.transpose(weight_bank[:], weight_blocks[:], identity[:])
@@ -116,14 +128,17 @@ def tile_picked_wema_tanh_lo_kernel(
             return kept
 
         w_codes = keep.tile([P, N], U32, name="w_codes", align_bytes=64)
-        w_plane = keep.tile([P, N], U8, name="w_plane", align_bytes=64)
+        w_plane = shared([P, N], U8, "w_plane", "w_plane")
         w_rounded = keep.tile([P, N * PACK], BF16, name="w_rounded", align_bytes=64)
         w_places = w_rounded[:].rearrange("p (t m j) -> p m j t", t=PACK, j=PACK)
         w_dealt = [w_raw[h][:].rearrange("p j (m t) -> p m j t", t=PACK) for h in range(2)]
         nc.vector.tensor_copy(w_places[:, :, 0:PAIR, :], w_dealt[0])
         groups = (slice(0, 1), slice(1, PAIR), slice(PAIR, PACK))
-        for copy, ts in zip((nc.vector.tensor_copy, nc.vector.tensor_copy, nc.scalar.copy), groups):
-            copy(w_places[:, :, PAIR:PACK, ts], w_dealt[1][:, :, :, ts])
+        for ts in groups[0:PAIR]:
+            nc.vector.tensor_copy(w_places[:, :, PAIR:PACK, ts], w_dealt[1][:, :, :, ts])
+        nc.scalar.activation(
+            w_places[:, :, PAIR:PACK, PAIR:PACK], w_dealt[1][:, :, :, PAIR:PACK], COPY, scale=round_unit[:]
+        )
         for ts in groups:
             cols = slice(ts.start * P, ts.stop * P)
             nc.vector.quantize_mx(
@@ -132,10 +147,10 @@ def tile_picked_wema_tanh_lo_kernel(
                 w_rounded[:, ts.start * P * PACK : ts.stop * P * PACK],
             )
 
-        kept0 = keep.tile([P, T], F32, name="kept0")
-        gather_times_old(0, kept0[:])
-        picked1 = keep.tile([P, T], F32, name="picked1")
-        gather_times_old(1, picked1[:])
+        kept_early = shared([P, PAIR * T], F32, "kept_early", "w_raw1")
+        kept0, picked1 = kept_early[:, 0:T], kept_early[:, T : 2 * T]
+        gather_times_old(0, kept0)
+        gather_times_old(1, picked1)
 
         moved = [keep.tile([P, T], F32, name="fresh_first"), keep.tile([P, T], F32, name="moved1")]
 

@@ -64,9 +64,11 @@ def tile_picked_wema_tanh_lo_kernel(
         identity = keep.tile([P, P], F32, name="identity")
 
         nc.gpsimd.memset(x_plane[:].bitcast(I32), 0)
-        old_cols = keep.tile([P, PACK], F32, name="old_cols")
-        nc.sync.dma_start(old_cols[:], old[0, :].rearrange("(q i) -> q i", i=PACK))
-        nc.sync.dma_start(weight_blocks[:], new[0 : P // BLOCKS, :].rearrange("r (b q) -> (r b) q", b=BLOCKS))
+        for h, weights in enumerate((old, new)):
+            nc.sync.dma_start(
+                weight_blocks[h * P // 2 : (h + 1) * P // 2, :],
+                weights[0 : P // 2 // BLOCKS, :].rearrange("r (b q) -> (r b) q", b=BLOCKS),
+            )
         nc.sync.dma_start(offsets[:], slot)
         w_rows = w1.rearrange("(p j) n -> p j n", j=PACK)
         for h in range(2):
@@ -84,8 +86,6 @@ def tile_picked_wema_tanh_lo_kernel(
         zero = keep.tile([P, 1], F32, name="zero")
         no_bias = shared([P, 1], F32, "no_bias", BIAS)
         nc.vector.memset(zero[:], 0.0)
-        lead_bias = shared([P, 1], F32, "lead_bias", LEADING)
-        nc.vector.memset(lead_bias[:], 0.0)
         spread_bias = shared([P, 1], F32, "spread_bias", "spread")
         nc.vector.memset(spread_bias[:], 0.0)
         spread_unit = shared([P, 1], F32, "spread_unit", "w_plane")
@@ -98,33 +98,30 @@ def tile_picked_wema_tanh_lo_kernel(
 
         make_identity(nc, identity[:])
 
-        old_bank = psum.tile([P, PACK, P], F32, name="old_bank", tag="turn", bufs=2)
-        for i in range(PACK):
-            nc.tensor.transpose(old_bank[:, i, :], old_cols[:, i : i + 1].to_broadcast([P, P]), identity[:])
-        nc.scalar.activation(
-            old_rows[:].rearrange("p (q i) -> p q i", i=PACK),
-            old_bank[:].rearrange("p i q -> p q i"),
-            IDENTITY,
-            bias=spread_bias[:],
-            scale=spread_unit[:],
-        )
-        round_unit = shared([P, 1], F32, "round_unit", "spread")
-        nc.scalar.copy(round_unit[:], unit[:])
-
         weight_bank = psum.tile([P, P], F32, name="weight_bank", tag="turn", bufs=2)
         nc.tensor.transpose(weight_bank[:], weight_blocks[:], identity[:])
-        new_cols = keep.tile([P, BLOCKS], F32, name="new_cols")
-        nc.scalar.copy(new_cols[:], weight_bank[:, 0:BLOCKS])
+        weight_cols = keep.tile([P, 2, BLOCKS], F32, name="weight_cols")
+        nc.scalar.copy(weight_cols[:], weight_bank[:].rearrange("p (h c) -> p h c", h=2)[:, :, 0:BLOCKS])
+        old_cols, new_cols = weight_cols[:, 0, :], weight_cols[:, 1, :]
+
+        old_bank = psum.tile([P, T], F32, name="old_bank", tag="turn", bufs=2)
+        for b in range(BLOCKS):
+            nc.tensor.transpose(old_bank[:, block(b)], old_cols[:, b : b + 1].to_broadcast([P, P]), identity[:])
+        nc.scalar.activation(old_rows[:], old_bank[:], IDENTITY, bias=spread_bias[:], scale=spread_unit[:])
+        lead_bank = psum.tile([P, LEAD], F32, name="lead_bank", tag="turn", bufs=2)
+        for b in range(LEAD // P):
+            nc.tensor.transpose(lead_bank[:, block(b)], new_cols[:, b : b + 1].to_broadcast([P, P]), identity[:])
 
         def gather_times_old(t, kept):
             nc.vector.tensor_tensor(kept, window[t][:].indirect(offsets[:]), old_rows[:], MULT)
 
         def times_old_turned(t, picked):
-            bank = psum.tile([P, BLOCKS, P], F32, name=f"picked_bank{t}", tag="sum0a")
+            bank = psum.tile([P, BLOCKS, P], F32, name=f"picked_bank{t}", tag="sum0b")
             for b in range(BLOCKS):
                 nc.tensor.transpose(bank[:, b, :], picked[:, block(b)], identity[:])
             kept = shared([P, BLOCKS, P], F32, f"kept{t}", FRESH)
-            nc.scalar.copy(kept[:], bank[:])
+            for b in range(BLOCKS):
+                nc.scalar.activation(kept[:, b, :], bank[:, b, :], COPY, scale=old_cols[:, b : b + 1])
             return kept
 
         w_codes = keep.tile([P, N], U32, name="w_codes", align_bytes=64)
@@ -134,11 +131,8 @@ def tile_picked_wema_tanh_lo_kernel(
         w_dealt = [w_raw[h][:].rearrange("p j (m t) -> p m j t", t=PACK) for h in range(2)]
         nc.vector.tensor_copy(w_places[:, :, 0:PAIR, :], w_dealt[0])
         groups = (slice(0, 1), slice(1, PAIR), slice(PAIR, PACK))
-        for ts in groups[0:PAIR]:
+        for ts in groups:
             nc.vector.tensor_copy(w_places[:, :, PAIR:PACK, ts], w_dealt[1][:, :, :, ts])
-        nc.scalar.activation(
-            w_places[:, :, PAIR:PACK, PAIR:PACK], w_dealt[1][:, :, :, PAIR:PACK], COPY, scale=round_unit[:]
-        )
         for ts in groups:
             cols = slice(ts.start * P, ts.stop * P)
             nc.vector.quantize_mx(
@@ -150,7 +144,9 @@ def tile_picked_wema_tanh_lo_kernel(
         kept_early = shared([P, PAIR * T], F32, "kept_early", "w_raw1")
         kept0, picked1 = kept_early[:, 0:T], kept_early[:, T : 2 * T]
         gather_times_old(0, kept0)
-        gather_times_old(1, picked1)
+        nc.vector.tensor_copy(picked1, window[1][:].indirect(offsets[:]))
+        new_lead = shared([P, LEAD], F32, "new_lead", "spread")
+        nc.scalar.copy(new_lead[:], lead_bank[:])
 
         moved = [keep.tile([P, T], F32, name="fresh_first"), keep.tile([P, T], F32, name="moved1")]
 
@@ -191,9 +187,21 @@ def tile_picked_wema_tanh_lo_kernel(
             entries = offsets[:, cols.start // 16 : cols.stop // 16]
             nc.vector.tensor_tensor(window[0][:].indirect(entries), kept0[:, cols], moved[0][:, cols], ADD)
 
-        blend_turned("0a", 0, list(range(LEAD // P)), [], "fresh0a", lead_bias)
+        acc_lead = psum.tile([P, LEAD], F32, name="acc_lead", tag="acc0a")
+        nc.tensor.matmul_mx(
+            out=acc_lead[:],
+            lhsT=w_codes[:, block(0)].bitcast(FP8X4),
+            lhsT_scale=w_plane[:, block(0)],
+            rhs=x_codes[:, 0:LEAD].bitcast(FP8X4),
+            rhs_scale=x_plane[:, 0:LEAD],
+            start=True,
+            stop=True,
+        )
+        y_lead = keep.tile([P, LEAD], F32, name="y_lead")
+        nc.scalar.activation(y_lead[:], acc_lead[:], TANH, bias=no_bias[:])
+        nc.gpsimd.tensor_tensor(moved[0][:, 0:LEAD], y_lead[:], new_lead[:], MULT)
         scatter_first(slice(0, LEAD))
-        kept_late = [shared([P, T], F32, "kept2", LEADING)]
+        kept_late = [shared([P, T], F32, "kept2", "spread")]
         gather_times_old(2, kept_late[0][:])
         blend_turned("0b", 0, list(range(LEAD // P, BLOCKS)), [], FRESH, rest_bias)
         scatter_first(slice(LEAD, T))
@@ -203,7 +211,7 @@ def tile_picked_wema_tanh_lo_kernel(
 
         y_pair = shared([P, PAIR, T], F32, "y_pair", TANHS)
         for i in range(PAIR):
-            acc = psum.tile([P, T], F32, name=f"acc{PAIR + i}", tag=("sum0b", "acc1")[i])
+            acc = psum.tile([P, T], F32, name=f"acc{PAIR + i}", tag=("acc0b", "acc1")[i])
             nc.tensor.matmul_mx(
                 out=acc[:],
                 lhsT=w_codes[:, block(PAIR + i)].bitcast(FP8X4),

@@ -9,7 +9,7 @@ PACK = 4
 QUADRANT = 32
 BLOCKS = T // P
 PAIR = 2
-LEAD = 256
+HALF = T // 2
 
 F32 = mybir.dt.float32
 BF16 = mybir.dt.bfloat16
@@ -23,12 +23,6 @@ ADD = mybir.AluOpType.add
 TANH = mybir.ActivationFunctionType.Tanh
 IDENTITY = mybir.ActivationFunctionType.Identity
 COPY = mybir.ActivationFunctionType.Copy
-
-BIAS = "bias"
-FIRST = "first"
-LEADING = "leading"
-TANHS = "tanhs"
-FRESH = "fresh"
 
 FLOPS = 2 * K * N * T
 BYTES = K * T + K * T // 32 + 4 * N * U + 4 * K * N + 2 * 4 * T + 2 * P * T // 16 + 4 * N * U + N * U + N * U // 32
@@ -55,12 +49,11 @@ def tile_picked_wema_tanh_lo_kernel(
 
         offsets = keep.tile([P, T // 16], U16, name="offsets")
         window = [keep.tile([P, U], F32, name=f"window{t}") for t in range(PACK)]
-        w_raw = [shared([P, PAIR, N], F32, f"w_raw{h}", f"w_raw{h}") for h in range(2)]
+        w_raw = [keep.tile([P, PAIR, N], F32, name=f"w_raw{h}") for h in range(2)]
         x_codes = keep.tile([P, T], U32, name="x_codes", align_bytes=64)
         x_plane = keep.tile([P, T], U8, name="x_plane", align_bytes=64)
         weight_blocks = keep.tile([P, P], F32, name="weight_blocks")
-        old_rows = reuse.tile([P, T], F32, name="old_rows", offset=0)
-        new_rows = keep.tile([P, T], F32, name="new_rows")
+        old_rows = keep.tile([P, T], F32, name="old_rows")
         identity = keep.tile([P, P], F32, name="identity")
 
         nc.gpsimd.memset(x_plane[:].bitcast(I32), 0)
@@ -81,189 +74,153 @@ def tile_picked_wema_tanh_lo_kernel(
         nc.sync.dma_start(x_codes[:].bitcast(I32), x_rows)
         for t in range(PACK):
             nc.sync.dma_start(window[t][:], mem_rows[:, t, :])
-        nc.sync.dma_start(new_rows[:], new)
 
         zero = keep.tile([P, 1], F32, name="zero")
-        no_bias = shared([P, 1], F32, "no_bias", BIAS)
+        no_bias = keep.tile([P, 1], F32, name="no_bias")
         nc.vector.memset(zero[:], 0.0)
-        spread_bias = shared([P, 1], F32, "spread_bias", "spread")
-        nc.vector.memset(spread_bias[:], 0.0)
         spread_unit = shared([P, 1], F32, "spread_unit", "w_plane")
         nc.vector.memset(spread_unit[:], 1.0)
-        unit = reuse.tile([P, 1], F32, name="unit", offset=4 * T)
-        nc.vector.memset(unit[:], 1.0)
-        rest_bias = shared([P, 1], F32, "rest_bias", "rest")
-        nc.vector.memset(rest_bias[:], 0.0)
         nc.scalar.activation(no_bias[:], zero[:], TANH)
 
         make_identity(nc, identity[:])
-
-        weight_bank = psum.tile([P, P], F32, name="weight_bank", tag="turn", bufs=2)
+        weight_bank = psum.tile([P, P], F32, name="weight_bank")
         nc.tensor.transpose(weight_bank[:], weight_blocks[:], identity[:])
         weight_cols = keep.tile([P, 2, BLOCKS], F32, name="weight_cols")
         nc.scalar.copy(weight_cols[:], weight_bank[:].rearrange("p (h c) -> p h c", h=2)[:, :, 0:BLOCKS])
-        old_cols, new_cols = weight_cols[:, 0, :], weight_cols[:, 1, :]
-
-        old_bank = psum.tile([P, T], F32, name="old_bank", tag="turn", bufs=2)
-        for b in range(BLOCKS):
-            nc.tensor.transpose(old_bank[:, block(b)], old_cols[:, b : b + 1].to_broadcast([P, P]), identity[:])
-        nc.scalar.activation(old_rows[:], old_bank[:], IDENTITY, bias=spread_bias[:], scale=spread_unit[:])
-        lead_bank = psum.tile([P, LEAD], F32, name="lead_bank", tag="turn", bufs=2)
-        for b in range(LEAD // P):
-            nc.tensor.transpose(lead_bank[:, block(b)], new_cols[:, b : b + 1].to_broadcast([P, P]), identity[:])
-
-        def gather_times_old(t, kept):
-            nc.vector.tensor_tensor(kept, window[t][:].indirect(offsets[:]), old_rows[:], MULT)
-
-        def times_old_turned(t, picked):
-            bank = psum.tile([P, BLOCKS, P], F32, name=f"picked_bank{t}", tag="sum0b")
+        old_bank = psum.tile([P, T], F32, name="old_bank")
+        new_bank = psum.tile([P, T], F32, name="new_bank")
+        for h, bank in enumerate((old_bank, new_bank)):
             for b in range(BLOCKS):
-                nc.tensor.transpose(bank[:, b, :], picked[:, block(b)], identity[:])
-            kept = shared([P, BLOCKS, P], F32, f"kept{t}", FRESH)
-            for b in range(BLOCKS):
-                nc.scalar.activation(kept[:, b, :], bank[:, b, :], COPY, scale=old_cols[:, b : b + 1])
-            return kept
+                nc.tensor.transpose(bank[:, block(b)], weight_cols[:, h, b : b + 1].to_broadcast([P, P]), identity[:])
+        nc.scalar.activation(old_rows[:], old_bank[:], COPY, scale=spread_unit[:])
 
         w_codes = keep.tile([P, N], U32, name="w_codes", align_bytes=64)
         w_plane = shared([P, N], U8, "w_plane", "w_plane")
-        w_rounded = keep.tile([P, N * PACK], BF16, name="w_rounded", align_bytes=64)
+        w_rounded = shared([P, N * PACK], BF16, "w_rounded", "w_rounded")
         w_places = w_rounded[:].rearrange("p (t m j) -> p m j t", t=PACK, j=PACK)
         w_dealt = [w_raw[h][:].rearrange("p j (m t) -> p m j t", t=PACK) for h in range(2)]
         nc.vector.tensor_copy(w_places[:, :, 0:PAIR, :], w_dealt[0])
         groups = (slice(0, 1), slice(1, PAIR), slice(PAIR, PACK))
-        for ts in groups:
+        def round_w(ts):
             nc.vector.tensor_copy(w_places[:, :, PAIR:PACK, ts], w_dealt[1][:, :, :, ts])
-        for ts in groups:
-            cols = slice(ts.start * P, ts.stop * P)
+
+        def quantise_w(ts):
             nc.vector.quantize_mx(
-                w_codes[:, cols].bitcast(FP8X4),
-                w_plane[:, cols],
+                w_codes[:, ts.start * P : ts.stop * P].bitcast(FP8X4),
+                w_plane[:, ts.start * P : ts.stop * P],
                 w_rounded[:, ts.start * P * PACK : ts.stop * P * PACK],
             )
 
-        kept_early = shared([P, PAIR * T], F32, "kept_early", "w_raw1")
-        kept0, picked1 = kept_early[:, 0:T], kept_early[:, T : 2 * T]
-        gather_times_old(0, kept0)
-        nc.vector.tensor_copy(picked1, window[1][:].indirect(offsets[:]))
-        new_lead = shared([P, LEAD], F32, "new_lead", "spread")
-        nc.scalar.copy(new_lead[:], lead_bank[:])
+        round_w(groups[0])
+        round_w(groups[1])
+        quantise_w(groups[0])
+        round_w(groups[2])
+        quantise_w(groups[1])
+        quantise_w(groups[2])
 
-        moved = [keep.tile([P, T], F32, name="fresh_first"), keep.tile([P, T], F32, name="moved1")]
+        halves = [slice(0, HALF), slice(HALF, T)]
+        whole = slice(0, T)
 
-        def blend_turned(name, t, blocks, kept, fresh_tag, bias, scale=1.0):
-            count = len(blocks)
-            acc = psum.tile([P, count, P], F32, name=f"acc{name}", tag=f"acc{name}")
-            for i, b in enumerate(blocks):
-                nc.tensor.matmul_mx(
-                    out=acc[:, i, :],
-                    lhsT=x_codes[:, block(b)].bitcast(FP8X4),
-                    lhsT_scale=x_plane[:, block(b)],
-                    rhs=w_codes[:, block(t)].bitcast(FP8X4),
-                    rhs_scale=w_plane[:, block(t)],
-                    start=True,
-                    stop=True,
-                )
-            y = shared([P, count, P], F32, f"y{name}", TANHS)
-            nc.scalar.activation(y[:], acc[:], TANH, bias=no_bias[:])
-            fresh = shared([P, count, P], F32, f"fresh{name}", fresh_tag)
-            for i, b in enumerate(blocks):
-                nc.scalar.activation(fresh[:, i, :], y[:, i, :], COPY, scale=new_cols[:, b : b + 1])
-            bank = psum.tile([P, count * P], F32, name=f"sum{name}", tag=f"sum{name}")
-            for i, b in enumerate(blocks):
-                terms = [fresh[:, i, :]] + [term[:, b, :] for term in kept]
-                for n, term in enumerate(terms):
-                    nc.tensor.matmul(
-                        bank[:, block(i)],
-                        term,
-                        identity[:],
-                        start=n == 0,
-                        stop=n == len(terms) - 1,
-                        is_transpose=True,
-                    )
-            cols = slice(blocks[0] * P, (blocks[-1] + 1) * P)
-            nc.scalar.activation(moved[t][:, cols], bank[:], IDENTITY, bias=bias[:], scale=scale)
-
-        def scatter_first(cols):
-            entries = offsets[:, cols.start // 16 : cols.stop // 16]
-            nc.vector.tensor_tensor(window[0][:].indirect(entries), kept0[:, cols], moved[0][:, cols], ADD)
-
-        acc_lead = psum.tile([P, LEAD], F32, name="acc_lead", tag="acc0a")
-        nc.tensor.matmul_mx(
-            out=acc_lead[:],
-            lhsT=w_codes[:, block(0)].bitcast(FP8X4),
-            lhsT_scale=w_plane[:, block(0)],
-            rhs=x_codes[:, 0:LEAD].bitcast(FP8X4),
-            rhs_scale=x_plane[:, 0:LEAD],
-            start=True,
-            stop=True,
-        )
-        y_lead = keep.tile([P, LEAD], F32, name="y_lead")
-        nc.scalar.activation(y_lead[:], acc_lead[:], TANH, bias=no_bias[:])
-        nc.gpsimd.tensor_tensor(moved[0][:, 0:LEAD], y_lead[:], new_lead[:], MULT)
-        scatter_first(slice(0, LEAD))
-        kept_late = [shared([P, T], F32, "kept2", "spread")]
-        gather_times_old(2, kept_late[0][:])
-        blend_turned("0b", 0, list(range(LEAD // P, BLOCKS)), [], FRESH, rest_bias)
-        scatter_first(slice(LEAD, T))
-        kept_late.append(shared([P, T], F32, "kept3", "rest"))
-        gather_times_old(3, kept_late[1][:])
-        blend_turned("1", 1, list(range(BLOCKS)), [times_old_turned(1, picked1)], "fresh1", no_bias, unit[:])
-
-        y_pair = shared([P, PAIR, T], F32, "y_pair", TANHS)
-        for i in range(PAIR):
-            acc = psum.tile([P, T], F32, name=f"acc{PAIR + i}", tag=("acc0b", "acc1")[i])
+        def project(name, t, cols, y):
+            acc = psum.tile([P, cols.stop - cols.start], F32, name=f"acc{name}")
             nc.tensor.matmul_mx(
                 out=acc[:],
-                lhsT=w_codes[:, block(PAIR + i)].bitcast(FP8X4),
-                lhsT_scale=w_plane[:, block(PAIR + i)],
-                rhs=x_codes[:].bitcast(FP8X4),
-                rhs_scale=x_plane[:],
+                lhsT=w_codes[:, block(t)].bitcast(FP8X4),
+                lhsT_scale=w_plane[:, block(t)],
+                rhs=x_codes[:, cols].bitcast(FP8X4),
+                rhs_scale=x_plane[:, cols],
                 start=True,
                 stop=True,
             )
-            nc.scalar.activation(y_pair[:, i, :], acc[:], TANH, bias=no_bias[:])
-        fresh_pair = reuse.tile([P, PAIR, T], F32, name="fresh_pair", offset=0)
-        nc.gpsimd.tensor_tensor(fresh_pair[:], y_pair[:], new_rows[:].unsqueeze(1).to_broadcast([P, PAIR, T]), MULT)
+            nc.scalar.activation(y, acc[:], TANH, bias=no_bias[:])
 
-        rounded = shared([P, U, PACK], BF16, "rounded", BIAS)
-        quarter = U // 4
-        split = U // 2
+        y0 = [keep.tile([P, HALF], F32, name=f"y0{h}") for h in range(2)]
+        y1 = shared([P, T], F32, "y1", "y1")
+        y2 = reuse.tile([P, T], F32, name="y2", offset=2 * T)
+        y3 = shared([P, T], F32, "y3", "y3")
+        for h in range(2):
+            project(f"0{h}", 0, halves[h], y0[h][:])
+        for t, y in ((1, y1), (2, y2), (3, y3)):
+            project(f"{t}", t, whole, y[:])
+
+        def entries(cols):
+            return offsets[:, cols.start // 16 : cols.stop // 16]
+
+        def gather(t, cols, kept):
+            nc.vector.tensor_tensor(kept[:], window[t][:].indirect(entries(cols)), old_rows[:, cols], MULT)
+
+        def weigh(fresh, y, cols):
+            nc.vector.tensor_tensor(fresh, y[:], new_bank[:, cols], MULT)
+
+        def add(name, tag, kept, fresh, width=HALF):
+            moved = shared([P, width], F32, name, tag)
+            nc.vector.tensor_tensor(moved[:], kept, fresh, ADD)
+            return moved
+
+        def scatter(t, cols, moved):
+            nc.scalar.activation(window[t][:].indirect(entries(cols)), moved[:], COPY)
+
+        first, second = halves
+        fresh0 = keep.tile([P, T], F32, name="fresh0")
+        fresh1 = keep.tile([P, T], F32, name="fresh1")
+        kept0a = shared([P, HALF], F32, "kept0a", "w_rounded")
+        kept0b = shared([P, HALF], F32, "kept0b", "kept0b")
+        gather(0, first, kept0a)
+        weigh(fresh0[:, first], y0[0], first)
+        gather(0, second, kept0b)
+        scatter(0, first, add("moved0a", "ring0", kept0a[:], fresh0[:, first]))
+        weigh(fresh0[:, second], y0[1], second)
+        weigh(fresh1[:], y1, whole)
+        scatter(0, second, add("moved0b", "ring1", kept0b[:], fresh0[:, second]))
+        kept1 = shared([P, T], F32, "kept1", "y1")
+        gather(1, whole, kept1)
+        fresh2 = shared([P, T], F32, "fresh2", "kept0b")
+        weigh(fresh2[:], y2, whole)
+        scatter(1, first, add("moved1a", "ring0", kept1[:, first], fresh1[:, first]))
+        kept2 = reuse.tile([P, T], F32, name="kept2", offset=0)
+        gather(2, whole, kept2)
+        fresh3 = reuse.tile([P, T], F32, name="fresh3", offset=4 * T)
+        weigh(fresh3[:], y3, whole)
+        scatter(2, first, add("moved2a", "ring1", kept2[:, first], fresh2[:, first]))
+        kept3 = shared([P, T], F32, "kept3", "y3")
+        gather(3, whole, kept3)
+        scatter(1, second, add("moved1b", "ring0", kept1[:, second], fresh1[:, second]))
+        moved3 = add("moved3", "moved3", kept3[:], fresh3[:], T)
+        scatter(2, second, add("moved2b", "ring1", kept2[:, second], fresh2[:, second]))
+        nc.vector.tensor_copy(window[3][:].indirect(offsets[:]), moved3[:])
         for t in range(PACK):
-            if t == 1:
-                nc.vector.tensor_copy(window[t][:].indirect(offsets[:]), moved[t][:])
-            elif t > 1:
-                nc.vector.tensor_tensor(
-                    window[t][:].indirect(offsets[:]), kept_late[t - PAIR][:], fresh_pair[:, t - PAIR, :], ADD
-                )
             nc.sync.dma_start(out_rows[:, t, :], window[t][:])
-            if t < PACK - 2:
-                nc.scalar.copy(rounded[:, :, t], window[t][:])
-            elif t == PACK - 2:
-                nc.scalar.copy(
-                    rounded[:, 0:split, t : t + 2], window[t][:, 0:split].unsqueeze(2).to_broadcast([P, split, 2])
-                )
-                nc.scalar.copy(rounded[:, split:U, t], window[t][:, split:U])
 
-        eighth = U // 8
-        chunks = [slice(0, split), slice(split, U - eighth), slice(U - eighth, U)]
-        for copy, cols in (
-            (nc.vector.tensor_copy, slice(0, quarter)),
-            (nc.vector.tensor_copy, slice(quarter, split)),
-            (nc.scalar.copy, slice(split, 3 * U // 4)),
-            (nc.scalar.copy, slice(3 * U // 4, U - eighth)),
-            (nc.scalar.copy, slice(U - eighth, U)),
-        ):
-            copy(rounded[:, cols, PACK - 1], window[PACK - 1][:, cols])
+        split = U // 2
+        sides = [slice(0, split), slice(split, U)]
+        pairs = [
+            shared([P, 2, cols.stop - cols.start, PAIR], BF16, f"pairs{s}", ("y3", "kept0b")[s])
+            for s, cols in enumerate(sides)
+        ]
+        for t in range(PAIR):
+            for s, cols in enumerate(sides):
+                nc.gpsimd.tensor_scalar(pairs[s][:, 0, :, t], window[t][:, cols], 1.0, -0.0, MULT, ADD)
+        for t in range(PAIR, PACK):
+            nc.vector.tensor_copy(pairs[0][:, 1, :, t - PAIR], window[t][:, sides[0]])
+            nc.scalar.copy(pairs[1][:, 1, :, t - PAIR], window[t][:, sides[1]])
+
         codes = keep.tile([P, U], U32, name="codes", align_bytes=64)
         plane = keep.tile([P, U], U8, name="plane", align_bytes=64)
         words = out_1[0].rearrange("p u j -> p (u j)").bitcast(I32)
-        edges = [0, quarter, 2 * quarter, 3 * quarter, U - eighth, U]
-        for start, stop in zip(edges, edges[1:]):
-            cols = slice(start, stop)
-            nc.vector.quantize_mx(
-                codes[:, cols].bitcast(FP8X4), plane[:, cols], rounded[:, cols, :].rearrange("p u j -> p (u j)")
+        quarter = U // 4
+        for c in range(4):
+            cols = slice(c * quarter, (c + 1) * quarter)
+            s = c // 2
+            rounded = keep.tile([P, quarter * PACK], BF16, name=f"rounded{c}", align_bytes=64)
+            dtype, copy = (I32, nc.vector.tensor_copy) if c < 3 else (U32, nc.scalar.copy)
+            source = pairs[s][:].rearrange("p h u e -> p h (u e)").bitcast(dtype)
+            local = slice(cols.start - sides[s].start, cols.stop - sides[s].start)
+            copy(
+                rounded[:].bitcast(dtype).rearrange("p (u h) -> p u h", h=2),
+                source[:, :, local].rearrange("p h u -> p u h"),
             )
-        for cols in chunks:
+            nc.vector.quantize_mx(codes[:, cols].bitcast(FP8X4), plane[:, cols], rounded[:])
+        for cols in (slice(0, split), slice(split, U - quarter), slice(U - quarter, U)):
             nc.sync.dma_start(words[:, cols], codes[:, cols].bitcast(I32))
         for q in range(P // QUADRANT):
             queue = nc.scalar if q % 2 == 0 else nc.sync

from contextlib import ExitStack

import concourse.mybir as mybir
from concourse.masks import make_identity

K, T, N, U = 512, 512, 512, 1024
P = 128
PACK = 4
QUADRANT = 32
BLOCKS = T // P
PAIR = 2
HALF = T // 2

F32 = mybir.dt.float32
BF16 = mybir.dt.bfloat16
I32 = mybir.dt.int32
U32 = mybir.dt.uint32
U16 = mybir.dt.uint16
U8 = mybir.dt.uint8
FP8X4 = mybir.dt.float8_e4m3fn_x4
MULT = mybir.AluOpType.mult
ADD = mybir.AluOpType.add
TANH = mybir.ActivationFunctionType.Tanh
IDENTITY = mybir.ActivationFunctionType.Identity
COPY = mybir.ActivationFunctionType.Copy

FLOPS = 2 * K * N * T
BYTES = K * T + K * T // 32 + 4 * N * U + 4 * K * N + 2 * 4 * T + 2 * P * T // 16 + 4 * N * U + N * U + N * U // 32


def block(b):
    return slice(b * P, (b + 1) * P)


def tile_picked_wema_tanh_lo_kernel(
    tc, x_words, x_scales, mem, w1, old, new, slot, out_0, out_1, out_2
):
    nc = tc.nc
    mem_rows = mem.rearrange("(p t) u -> p t u", t=PACK)
    out_rows = out_0.rearrange("(p t) u -> p t u", t=PACK)

    with ExitStack() as ctx:
        keep = ctx.enter_context(tc.tile_pool(name="keep", bufs=1))
        reuse = ctx.enter_context(tc.tile_pool(name="reuse", bufs=1))
        psum = ctx.enter_context(tc.psum_pool(name="psum", bufs=1))

        def shared(shape, dtype, name, tag):
            return keep.tile(shape, dtype, name=name, tag=tag, align_bytes=64)

        offsets = keep.tile([P, T // 16], U16, name="offsets")
        window = [keep.tile([P, U], F32, name=f"window{t}") for t in range(PACK)]
        w_raw = [keep.tile([P, PAIR, N], F32, name=f"w_raw{h}") for h in range(2)]
        x_codes = keep.tile([P, T], U32, name="x_codes", align_bytes=64)
        x_plane = keep.tile([P, T], U8, name="x_plane", align_bytes=64)
        weight_blocks = keep.tile([P, P], F32, name="weight_blocks")
        old_rows = keep.tile([P, T], F32, name="old_rows")
        identity = keep.tile([P, P], F32, name="identity")

        nc.gpsimd.memset(x_plane[:].bitcast(I32), 0)
        for h, weights in enumerate((old, new)):
            nc.sync.dma_start(
                weight_blocks[h * P // 2 : (h + 1) * P // 2, :],
                weights[0 : P // 2 // BLOCKS, :].rearrange("r (b q) -> (r b) q", b=BLOCKS),
            )
        nc.sync.dma_start(offsets[:], slot)
        w_rows = w1.rearrange("(p j) n -> p j n", j=PACK)
        for h in range(2):
            nc.sync.dma_start(w_raw[h][:], w_rows[:, PAIR * h : PAIR * (h + 1), :])
        for q in range(P // QUADRANT):
            nc.sync.dma_start(
                x_plane[QUADRANT * q : QUADRANT * q + 4, :].bitcast(I32), x_scales[0, 4 * q : 4 * q + 4, :].bitcast(I32)
            )
        x_rows = x_words[0].rearrange("p n j -> p (n j)").bitcast(I32)
        nc.sync.dma_start(x_codes[:].bitcast(I32), x_rows)
        for t in range(PACK):
            nc.sync.dma_start(window[t][:], mem_rows[:, t, :])

        zero = keep.tile([P, 1], F32, name="zero")
        no_bias = keep.tile([P, 1], F32, name="no_bias")
        nc.vector.memset(zero[:], 0.0)
        spread_unit = shared([P, 1], F32, "spread_unit", "w_plane")
        nc.vector.memset(spread_unit[:], 1.0)
        nc.scalar.activation(no_bias[:], zero[:], TANH)

        make_identity(nc, identity[:])
        weight_bank = psum.tile([P, P], F32, name="weight_bank")
        nc.tensor.transpose(weight_bank[:], weight_blocks[:], identity[:])
        weight_cols = keep.tile([P, 2, BLOCKS], F32, name="weight_cols")
        nc.scalar.copy(weight_cols[:], weight_bank[:].rearrange("p (h c) -> p h c", h=2)[:, :, 0:BLOCKS])
        old_bank = psum.tile([P, T], F32, name="old_bank")
        new_bank = psum.tile([P, T], F32, name="new_bank")
        for h, bank in enumerate((old_bank, new_bank)):
            for b in range(BLOCKS):
                nc.tensor.transpose(bank[:, block(b)], weight_cols[:, h, b : b + 1].to_broadcast([P, P]), identity[:])
        nc.scalar.activation(old_rows[:], old_bank[:], COPY, scale=spread_unit[:])

        w_codes = keep.tile([P, N], U32, name="w_codes", align_bytes=64)
        w_plane = shared([P, N], U8, "w_plane", "w_plane")
        w_rounded = shared([P, N * PACK], BF16, "w_rounded", "w_rounded")
        w_places = w_rounded[:].rearrange("p (t m j) -> p m j t", t=PACK, j=PACK)
        w_dealt = [w_raw[h][:].rearrange("p j (m t) -> p m j t", t=PACK) for h in range(2)]
        nc.vector.tensor_copy(w_places[:, :, 0:PAIR, :], w_dealt[0])
        groups = (slice(0, 1), slice(1, PAIR), slice(PAIR, PACK))
        def round_w(ts):
            nc.vector.tensor_copy(w_places[:, :, PAIR:PACK, ts], w_dealt[1][:, :, :, ts])

        def quantise_w(ts):
            nc.vector.quantize_mx(
                w_codes[:, ts.start * P : ts.stop * P].bitcast(FP8X4),
                w_plane[:, ts.start * P : ts.stop * P],
                w_rounded[:, ts.start * P * PACK : ts.stop * P * PACK],
            )

        round_w(groups[0])
        round_w(groups[1])
        quantise_w(groups[0])
        round_w(groups[2])
        quantise_w(groups[1])
        quantise_w(groups[2])

        halves = [slice(0, HALF), slice(HALF, T)]
        whole = slice(0, T)

        def project(name, t, cols, y):
            acc = psum.tile([P, cols.stop - cols.start], F32, name=f"acc{name}")
            nc.tensor.matmul_mx(
                out=acc[:],
                lhsT=w_codes[:, block(t)].bitcast(FP8X4),
                lhsT_scale=w_plane[:, block(t)],
                rhs=x_codes[:, cols].bitcast(FP8X4),
                rhs_scale=x_plane[:, cols],
                start=True,
                stop=True,
            )
            nc.scalar.activation(y, acc[:], TANH, bias=no_bias[:])

        y0 = [keep.tile([P, HALF], F32, name=f"y0{h}") for h in range(2)]
        y1 = shared([P, T], F32, "y1", "y1")
        y2 = reuse.tile([P, T], F32, name="y2", offset=2 * T)
        y3 = shared([P, T], F32, "y3", "y3")
        for h in range(2):
            project(f"0{h}", 0, halves[h], y0[h][:])
        for t, y in ((1, y1), (2, y2), (3, y3)):
            project(f"{t}", t, whole, y[:])

        def entries(cols):
            return offsets[:, cols.start // 16 : cols.stop // 16]

        def gather(t, cols, kept):
            nc.vector.tensor_tensor(kept[:], window[t][:].indirect(entries(cols)), old_rows[:, cols], MULT)

        def weigh(fresh, y, cols):
            nc.vector.tensor_tensor(fresh, y[:], new_bank[:, cols], MULT)

        def add(name, tag, kept, fresh, width=HALF):
            moved = shared([P, width], F32, name, tag)
            nc.vector.tensor_tensor(moved[:], kept, fresh, ADD)
            return moved

        def scatter(t, cols, moved):
            nc.scalar.activation(window[t][:].indirect(entries(cols)), moved[:], COPY)

        first, second = halves
        fresh0 = keep.tile([P, T], F32, name="fresh0")
        fresh1 = keep.tile([P, T], F32, name="fresh1")
        kept0a = shared([P, HALF], F32, "kept0a", "w_rounded")
        kept0b = shared([P, HALF], F32, "kept0b", "kept0b")
        gather(0, first, kept0a)
        weigh(fresh0[:, first], y0[0], first)
        gather(0, second, kept0b)
        scatter(0, first, add("moved0a", "ring0", kept0a[:], fresh0[:, first]))
        weigh(fresh0[:, second], y0[1], second)
        weigh(fresh1[:], y1, whole)
        scatter(0, second, add("moved0b", "ring1", kept0b[:], fresh0[:, second]))
        kept1 = shared([P, T], F32, "kept1", "y1")
        gather(1, whole, kept1)
        fresh2 = shared([P, T], F32, "fresh2", "kept0b")
        weigh(fresh2[:], y2, whole)
        scatter(1, first, add("moved1a", "ring0", kept1[:, first], fresh1[:, first]))
        kept2 = reuse.tile([P, T], F32, name="kept2", offset=0)
        gather(2, whole, kept2)
        fresh3 = reuse.tile([P, T], F32, name="fresh3", offset=4 * T)
        weigh(fresh3[:], y3, whole)
        scatter(2, first, add("moved2a", "ring1", kept2[:, first], fresh2[:, first]))
        kept3 = shared([P, T], F32, "kept3", "y3")
        gather(3, whole, kept3)
        scatter(1, second, add("moved1b", "ring0", kept1[:, second], fresh1[:, second]))
        moved3 = add("moved3", "moved3", kept3[:], fresh3[:], T)
        scatter(2, second, add("moved2b", "ring1", kept2[:, second], fresh2[:, second]))
        nc.vector.tensor_copy(window[3][:].indirect(offsets[:]), moved3[:])
        for t in range(PACK):
            nc.sync.dma_start(out_rows[:, t, :], window[t][:])

        split = U // 2
        sides = [slice(0, split), slice(split, U)]
        pairs = [
            shared([P, 2, cols.stop - cols.start, PAIR], BF16, f"pairs{s}", ("y3", "kept0b")[s])
            for s, cols in enumerate(sides)
        ]
        for t in range(PAIR):
            for s, cols in enumerate(sides):
                nc.gpsimd.tensor_scalar(pairs[s][:, 0, :, t], window[t][:, cols], 1.0, -0.0, MULT, ADD)
        for t in range(PAIR, PACK):
            nc.vector.tensor_copy(pairs[0][:, 1, :, t - PAIR], window[t][:, sides[0]])
            nc.scalar.copy(pairs[1][:, 1, :, t - PAIR], window[t][:, sides[1]])

        codes = keep.tile([P, U], U32, name="codes", align_bytes=64)
        plane = keep.tile([P, U], U8, name="plane", align_bytes=64)
        words = out_1[0].rearrange("p u j -> p (u j)").bitcast(I32)
        quarter = U // 4
        for c in range(4):
            cols = slice(c * quarter, (c + 1) * quarter)
            s = c // 2
            rounded = keep.tile([P, quarter * PACK], BF16, name=f"rounded{c}", align_bytes=64)
            dtype, copy = (I32, nc.vector.tensor_copy) if c < 3 else (U32, nc.scalar.copy)
            source = pairs[s][:].rearrange("p h u e -> p h (u e)").bitcast(dtype)
            local = slice(cols.start - sides[s].start, cols.stop - sides[s].start)
            copy(
                rounded[:].bitcast(dtype).rearrange("p (u h) -> p u h", h=2),
                source[:, :, local].rearrange("p h u -> p u h"),
            )
            nc.vector.quantize_mx(codes[:, cols].bitcast(FP8X4), plane[:, cols], rounded[:])
        for cols in (slice(0, split), slice(split, U - quarter), slice(U - quarter, U)):
            nc.sync.dma_start(words[:, cols], codes[:, cols].bitcast(I32))
        for q in range(P // QUADRANT):
            queue = nc.scalar if q % 2 == 0 else nc.sync
            queue.dma_start(
                out_2[0, 4 * q : 4 * q + 4, :].bitcast(I32), plane[QUADRANT * q : QUADRANT * q + 4, :].bitcast(I32)
            )
